import numpy as np
import ml_dtypes


def mxq(x, axis, fmt="e4m3"):
    dtype, down = {"e4m3": (ml_dtypes.float8_e4m3fn, 7), "e5m2": (ml_dtypes.float8_e5m2, 14)}[fmt]
    v = np.moveaxis(np.asarray(x, np.float32).astype(ml_dtypes.bfloat16).astype(np.float64), axis, -1)
    blocks = v.reshape(v.shape[:-1] + (-1, 32))
    amax = np.abs(blocks).max(-1, keepdims=True)
    byte = np.maximum(np.where(amax > 0, np.frexp(amax)[1] - 1 + 127, 0) - down, 1)
    scale = np.exp2(byte - 127.0)
    codes = (blocks / scale).astype(np.float32).astype(dtype).astype(np.float64)
    return np.moveaxis((codes * scale).reshape(v.shape), -1, axis)


WIDE = False


def mx_kscale(k):
    if not WIDE:
        return np.ones(k)
    levels = np.array([10, -10, 5, -5, 0])
    if k % 512:
        return np.exp2(np.random.permutation(np.resize(levels, k // 32))).repeat(32)
    a = np.empty((k // 512, 16))
    for p in range(k // 512):
        a[p, :8] = np.random.permutation(np.resize(levels, 8))
        for g in range(8):
            far = levels[np.abs(levels - a[p, g]) >= 10]
            a[p, g + 8] = far[np.random.randint(len(far))]
    return np.exp2(a.ravel()).repeat(32)


BF16 = ml_dtypes.bfloat16


def bf(x):
    return np.asarray(x, np.float32).astype(BF16)


def f64(x):
    return np.asarray(x).astype(np.float64)

def planes(Y):
    n, m = Y.shape
    b = f64(bf(Y)).reshape(n // 32, 32, m)
    amax = np.abs(b).max(1)
    byte = np.clip(np.where(amax > 0, np.frexp(amax)[1] - 1 + 127 - 7, 1), 1, 254)
    codes = (b * np.exp2(127.0 - byte)[:, None, :]).reshape(n, m).astype(np.float32).astype(ml_dtypes.float8_e4m3fn).view(np.uint8)
    words = codes.reshape(n // 512, 128, 4, m).transpose(0, 1, 3, 2)
    return np.ascontiguousarray(words), np.ascontiguousarray(byte.astype(np.uint8).reshape(n // 512, 16, m))


P, N, M, D, K = 4, 1024, 1024, 512, 512


def silu(t):
    return t / (1.0 + np.exp(-t))


def setup_inputs():
    s, t = mx_kscale(D), mx_kscale(K)
    u = np.random.standard_normal((N, D)) * s[None, :]
    w = np.random.standard_normal((P, D, K)) / np.sqrt(D) / s[None, :, None] * t[None, None, :]
    v = np.random.standard_normal((P, M, K)) / np.sqrt(K) / t[None, None, :]
    a = np.random.standard_normal((N, P))
    b = np.random.standard_normal((M, P))
    c = 1.0 + 0.5 * np.random.standard_normal(P)
    return {"u": bf(u), "w": bf(w), "v": bf(v), "a": bf(a), "b": bf(b), "c": bf(c)}


def core(u, w, v, a, b, c):
    q = mxq(f64(u), 1, "e4m3") @ mxq(f64(w), 1, "e4m3")
    l = mxq(q, 2, "e4m3") @ mxq(f64(v), 2, "e4m3").transpose(0, 2, 1)
    ab = f64(a).T[:, :, None] * f64(b).T[:, None, :]
    g = silu(ab + f64(c)[:, None, None] * l)
    e = np.exp(g - g.max(axis=0, keepdims=True))
    pi = e / e.sum(axis=0, keepdims=True)
    return np.sum(pi * l, axis=0)


def reference(u, w, v, a, b, c):
    R_out = core(u, w, v, a, b, c)
    words, scales = planes(R_out.T)
    return R_out, words, scales

@@ -1,0 +1,460 @@
+from contextlib import ExitStack
+
+import concourse.mybir as mybir
+from concourse.masks import make_identity
+
+F32 = mybir.dt.float32
+BF16 = mybir.dt.bfloat16
+U32 = mybir.dt.uint32
+I32 = mybir.dt.int32
+U8 = mybir.dt.uint8
+FP8X4 = mybir.dt.float8_e4m3fn_x4
+ALU = mybir.AluOpType
+ACT = mybir.ActivationFunctionType
+
+NP = 4
+N = 1024
+M = 1024
+D = 512
+K = 512
+FLOPS = 2 * NP * N * D * K + 2 * NP * N * M * K
+WINDOW = 32.0
+VEC_SUB = {"d": 2}
+PLAN = [(0, 0, 512, "d"), (0, 512, 512, "d"), (1, 512, 512, "d"), (1, 0, 512, "d")]
+LBUFS = {"lg": 2, "lw": 2, "s": 4, "e": 0}
+
+
+def tile_mixtureoflogitsretrievalscore_x1_kernel(tc, u, w, v, a, b, c, out, out_words, out_scales):
+    nc = tc.nc
+    with ExitStack() as ctx:
+        keep = ctx.enter_context(tc.tile_pool(name="keep", bufs=1))
+        sb = ctx.enter_context(tc.tile_pool(name="sb", bufs=2))
+        ps = ctx.enter_context(tc.psum_pool(name="ps", bufs=2))
+        with tc.tile_pool(name="pro", bufs=1) as pro:
+            ctx.enter_context(tc.manual_schedule(engines={mybir.EngineType.Activation}))
+            pool_of = {}
+
+            def bank(tag):
+                t = ps.tile([128, 512], F32, name=tag, tag=tag, bufs=LBUFS[tag])
+                return t
+
+            ident = keep.tile([128, 128], F32)
+            make_identity(nc, ident[:])
+            window = keep.tile([128, 1], F32)
+            nc.gpsimd.memset(window[:], WINDOW)
+
+            c_b = keep.tile([128, NP], BF16)
+            nc.scalar.dma_start(out=c_b[:], in_=c.partition_broadcast(128))
+            b_b = keep.tile([128, 2, 16], BF16)
+            nc.scalar.dma_start(out=b_b[:], in_=b.rearrange("(g p t) c -> p g (t c)", p=128, t=4))
+            a_b = keep.tile([128, 8, NP], BF16)
+            nc.scalar.dma_start(out=a_b[:], in_=a.rearrange("(i p) c -> p i c", p=128))
+
+            raws = {}
+
+            def load(key, src):
+                t = pro.tile([128, 4, 512], BF16, name="raw", tag="raw", bufs=5)
+                nc.sync.dma_start(out=t[:], in_=src)
+                raws[key] = t
+
+            def load_u(h):
+                load(("u", h), u[512 * h : 512 * h + 512, :].rearrange("(i p) d -> p i d", p=128))
+
+            def load_w(p):
+                load(("w", p), w[p].rearrange("(p j) c -> p j c", j=4))
+
+            def load_v(p, g):
+                load(("v", p, g), v[p, 512 * g : 512 * g + 512, :].rearrange("(p t) k -> p t k", t=4))
+
+            load_u(0)
+            load_w(0)
+            load_v(0, 0)
+            a_raw = pro.tile([128, N, NP], BF16)
+            nc.sync.dma_start(out=a_raw[:].rearrange("q n p -> q (n p)"), in_=a.rearrange("n p -> (n p)").partition_broadcast(128))
+            for p in range(1, NP):
+                load_w(p)
+                load_v(p, 0)
+                if p == 1:
+                    load_u(1)
+            for p in range(NP):
+                load_v(p, 1)
+
+            c_f = keep.tile([128, NP], F32)
+            nc.vector.tensor_copy(out=c_f[:], in_=c_b[:])
+            b_f = keep.tile([128, 32], F32)
+            nc.vector.tensor_copy(out=b_f[:], in_=b_b[:].rearrange("p g x -> p (g x)"))
+            a_f = keep.tile([128, 32], F32)
+            nc.vector.tensor_copy(out=a_f[:], in_=a_b[:].rearrange("p g x -> p (g x)"))
+
+            u_q = pro.tile([128, N], U32, align_bytes=64)
+            u_s = pro.tile([128, N], U8, align_bytes=64)
+            w_q = pro.tile([128, NP, K], U32, align_bytes=64)
+            w_s = pro.tile([128, NP, K], U8, align_bytes=64)
+            q_q = keep.tile([128, NP, N], U32, align_bytes=64)
+            q_s = keep.tile([128, NP, N], U8, align_bytes=64)
+            v_q = keep.tile([128, NP, M], U32, align_bytes=64)
+            v_s = keep.tile([128, NP, M], U8, align_bytes=64)
+            a_bc = keep.tile([128, NP, N], BF16)
+
+            def grp_tile(pool):
+                t = pool.tile([128, 512, 4], BF16, name="grp", tag="grp", bufs=4 if pool is pro else 2, align_bytes=64)
+                return t
+
+            def words_of(grp):
+                return grp[:].rearrange("p n f -> p (n f)").bitcast(F32).rearrange("p (i n u) -> p i n u", n=128, u=2)
+
+            def copy(eng, dst, src):
+                if eng == "g":
+                    nc.gpsimd.tensor_scalar(out=dst, in0=src, scalar1=1.0, scalar2=0.0, op0=ALU.mult, op1=ALU.add)
+                elif eng == "v":
+                    nc.vector.tensor_copy(out=dst, in_=src)
+                else:
+                    nc.scalar.copy(out=dst, in_=src)
+
+            def quantize(codes, scales, grp):
+                nc.vector.quantize_mx(out=codes.bitcast(FP8X4), scales=scales, in_=grp.rearrange("p n f -> p (n f)"))
+
+            tags = ["s"]
+
+            def next_tag():
+                tags.append(tags.pop(0))
+                return tags[0]
+
+            def turn(raw, engs):
+                grp = grp_tile(pro)
+                rw = raw[:].rearrange("p i k -> p (i k)").bitcast(F32)
+                gw = words_of(grp)
+                for half in range(2):
+                    xt = bank(next_tag())
+                    xv = xt[:].rearrange("p (i u n) -> p i u n", i=2, u=2)
+                    for i in range(2):
+                        for e in range(2):
+                            base = 256 * (2 * half + i)
+                            nc.tensor.transpose(xv[:, i, e, :], rw[:, base + e : base + 256 : 2], ident[:])
+                    copy(engs[half], gw[:, 2 * half : 2 * half + 2], xv.rearrange("p i u n -> p i n u"))
+                return grp
+
+            def prep_w(p, eng):
+                g_w = grp_tile(pro)
+                dst = g_w[:].rearrange("p x f -> p (x f)").rearrange("p (t m j) -> p t m j", t=4, j=4)
+                src = raws[("w", p)][:].rearrange("p j (m t) -> p t m j", t=4)
+                copy(eng, dst, src)
+                quantize(w_q[:, p, :], w_s[:, p, :], g_w[:])
+
+            def prep_u(h, engs):
+                grp = turn(raws[("u", h)], engs)
+                quantize(u_q[:, 512 * h : 512 * h + 512], u_s[:, 512 * h : 512 * h + 512], grp[:])
+
+            def prep_q(p, h, engs):
+                grp = grp_tile(pro)
+                for nb in range(4):
+                    acc = bank(next_tag())
+                    n0 = 512 * h + 128 * nb
+                    av = acc[:].rearrange("p (t n) -> p t n", t=4)
+                    for t in range(4):
+                        nc.tensor.matmul_mx(
+                            out=av[:, t, :],
+                            lhsT=w_q[:, p, 128 * t : 128 * t + 128].bitcast(FP8X4),
+                            lhsT_scale=w_s[:, p, 128 * t : 128 * t + 128],
+                            rhs=u_q[:, n0 : n0 + 128].bitcast(FP8X4),
+                            rhs_scale=u_s[:, n0 : n0 + 128],
+                            start=True,
+                            stop=True,
+                        )
+                    copy(engs[nb], grp[:, 128 * nb : 128 * nb + 128, :], av.rearrange("p t n -> p n t"))
+                quantize(q_q[:, p, 512 * h : 512 * h + 512], q_s[:, p, 512 * h : 512 * h + 512], grp[:])
+
+            def prep_v(p, g, engs):
+                grp = turn(raws[("v", p, g)], engs)
+                quantize(v_q[:, p, 512 * g : 512 * g + 512], v_s[:, p, 512 * g : 512 * g + 512], grp[:])
+
+            X = {}
+            EL = {}
+            AB = {}
+            C = {}
+            SH = {}
+            M2 = {}
+            RZ = {}
+            RB = {}
+            GR = {}
+
+            def mx(acc, st, st_s, s0, mv, mv_s, m0, wd, p):
+                nc.tensor.matmul_mx(
+                    out=acc,
+                    lhsT=st[:, p, s0 : s0 + 128].bitcast(FP8X4),
+                    lhsT_scale=st_s[:, p, s0 : s0 + 128],
+                    rhs=mv[:, p, m0 : m0 + wd].bitcast(FP8X4),
+                    rhs_scale=mv_s[:, p, m0 : m0 + wd],
+                    start=True,
+                    stop=True,
+                )
+
+            def open_x(k, t):
+                if k % 3 == 2:
+                    x = pool_of["late"].tile([128, NP, 512], F32, name="xb", tag="xb", bufs=4)
+                else:
+                    x = sb.tile([128, NP, 512], F32, name="x", tag="x", bufs=8)
+                X[(k, t)] = x
+
+            def cells(k):
+                g, n0, wd, route = PLAN[k]
+                return 4 if route == "d" else wd // 128
+
+            def products(k, i, p):
+                g, n0, wd, route = PLAN[k]
+                ab = sb.tile([128, 512], F32, name="ab", tag="ab", bufs=6)
+                if route == "d":
+                    col = 16 * g + 4 * i + p
+                    src, sc, width = a_bc[:, p, n0 : n0 + wd], b_f[:, col : col + 1], wd
+                else:
+                    src, sc, width = None, None, 512
+                AB[(k, i, p)] = ab
+                nc.gpsimd.tensor_scalar(out=ab[:, :width], in0=src, scalar1=sc, scalar2=-WINDOW, op0=ALU.mult, op1=ALU.add)
+
+            def cell_of(k, i):
+                g, n0, wd, route = PLAN[k]
+                if route == "d":
+                    return X[(k, i)][:, :, :wd]
+                if (k, i) not in C:
+                    xn = sb.tile([128, NP, 512], F32, name="xn", tag="xn", bufs=2)
+                    C[(k, i)] = xn
+                return C[(k, i)][:]
+
+            def argument(k, i, p):
+                g, n0, wd, route = PLAN[k]
+                acc = bank("lg")
+                if route == "d":
+                    width = wd
+                    mx(acc[:, :wd], v_q, v_s, 512 * g + 128 * i, q_q, q_s, n0, wd, p)
+                else:
+                    width = 512
+                    mx(acc[:], q_q, q_s, n0 + 128 * i, v_q, v_s, 512 * g, 512, p)
+                nc.vector.scalar_tensor_tensor(
+                    out=cell_of(k, i)[:, p, :], in0=acc[:, :width], scalar=c_f[:, p : p + 1], in1=AB[(k, i, p)][:, :width], op0=ALU.mult, op1=ALU.add
+                )
+
+            def max_a(k, i):
+                x = cell_of(k, i)
+                wd = PLAN[k][2] if PLAN[k][3] == "d" else 512
+                m2 = sb.tile([128, 2, 512], F32, name="m2", tag="m2", bufs=1)
+                M2[(k, i)] = m2
+                nc.vector.tensor_tensor(out=m2[:, :, :wd], in0=x[:, 0:2, :], in1=x[:, 2:4, :], op=ALU.max)
+
+            def max_b(k, i):
+                m2 = M2[(k, i)]
+                wd = PLAN[k][2] if PLAN[k][3] == "d" else 512
+                s = sb.tile([128, 512], F32, name="s", tag="shift", bufs=2)
+                SH[(k, i)] = s
+                nc.vector.scalar_tensor_tensor(out=s[:, :wd], in0=m2[:, 0, :wd], scalar=0.0, in1=m2[:, 1, :wd], op0=ALU.max, op1=ALU.max)
+                if PLAN[k][3] != "d":
+                    nc.vector.tensor_scalar(out=s[:], in0=s[:], scalar1=-1.0, scalar2=0.0, op0=ALU.mult, op1=ALU.add)
+
+            def shift_silu(k, i):
+                g, n0, wd, route = PLAN[k]
+                x = cell_of(k, i)
+                if route == "d":
+                    for p in range(NP):
+                        eng = nc.vector if p < VEC_SUB["d"] else nc.gpsimd
+                        eng.tensor_tensor(out=x[:, p, :], in0=x[:, p, :], in1=SH[(k, i)][:, :wd], op=ALU.subtract)
+                    nc.scalar.activation(out=x, in_=x, func=ACT.Silu, bias=window[:], scale=1.0)
+                else:
+                    for t in range(4):
+                        acc = bank("e")
+                        blk = slice(128 * t, 128 * t + 128)
+                        for p in range(NP):
+                            quarter = acc[:, 128 * p : 128 * p + 128]
+                            nc.tensor.matmul(out=quarter, lhsT=x[:, p, blk], rhs=ident[:], is_transpose=True, start=True, stop=False)
+                            nc.tensor.matmul(out=quarter, lhsT=SH[(k, i)][:, blk], rhs=ident[:], is_transpose=True, start=False, stop=True)
+                        nc.scalar.activation(
+                            out=X[(k, t)][:, :, 128 * i : 128 * i + 128],
+                            in_=acc[:].rearrange("m (p n) -> m p n", p=NP),
+                            func=ACT.Silu,
+                            bias=window[:],
+                            scale=1.0,
+                        )
+
+            def expo(k, t):
+                x = X[(k, t)][:, :, : PLAN[k][2]]
+                nc.scalar.activation(out=x, in_=x, func=ACT.Exp)
+
+            def weigh(k, t, p):
+                g, n0, wd, route = PLAN[k]
+                if p == 0:
+                    el = pool_of["late"].tile([128, NP, 512], F32, name="el", tag="el", bufs=4)
+                    EL[(k, t)] = el
+                acc = bank("lw")
+                mx(acc[:, :wd], v_q, v_s, 512 * g + 128 * t, q_q, q_s, n0, wd, p)
+                nc.vector.tensor_tensor(out=EL[(k, t)][:, p, :wd], in0=acc[:, :wd], in1=X[(k, t)][:, p, :wd], op=ALU.mult)
+
+            def sum_up(x, k, j):
+                acc = bank("s")
+                for t in range(4):
+                    for p in range(NP):
+                        nc.tensor.matmul(
+                            out=acc[:, 128 * t : 128 * t + 128],
+                            lhsT=x[(k, t)][:, p, 128 * j : 128 * j + 128],
+                            rhs=ident[:],
+                            is_transpose=True,
+                            start=(p == 0),
+                            stop=(p == NP - 1),
+                        )
+                return acc
+
+            def recip_a(k, j):
+                z = sum_up(X, k, j)
+                rz = sb.tile([128, 512], F32, name="rz", tag="rz", bufs=4)
+                RZ[(k, j)] = rz
+                nc.scalar.activation(out=rz[:].rearrange("n (p t) -> n p t", t=4), in_=z[:].rearrange("n (t p) -> n p t", t=4), func=ACT.Ln)
+
+            def recip_b(k, j):
+                rz = RZ[(k, j)]
+                nc.scalar.activation(out=rz[:], in_=rz[:], func=ACT.Exp, scale=-1.0)
+
+            def mix(k, j):
+                g, nn, wd, route = PLAN[k]
+                num = sum_up(EL, k, j)
+                r = sb.tile([128, 512], F32, name="r", tag="r", bufs=2)
+                nc.vector.tensor_tensor(
+                    out=r[:].rearrange("n (p t) -> n p t", t=4),
+                    in0=num[:].rearrange("n (t p) -> n p t", t=4),
+                    in1=RZ[(k, j)][:].rearrange("n (p t) -> n p t", t=4),
+                    op=ALU.mult,
+                )
+                n0 = nn + 128 * j
+                nc.sync.dma_start(out=out[n0 : n0 + 128, 512 * g : 512 * g + 512], in_=r[:])
+                rb = sb.tile([128, 2, 128, 2], BF16, name="rb", tag="rb", bufs=2)
+                RB[(k, j)] = rb
+                nc.gpsimd.tensor_scalar(
+                    out=rb[:], in0=r[:].rearrange("n (p u e) -> n u p e", u=2, e=2), scalar1=1.0, scalar2=0.0, op0=ALU.mult, op1=ALU.add
+                )
+
+            def planes_turn(k, half):
+                if half == 0:
+                    GR[k] = grp_tile(sb)
+                gw = words_of(GR[k])
+                xt = bank("s")
+                xv = xt[:].rearrange("p (i u n) -> p i u n", i=2, u=2)
+                for i in range(2):
+                    rbw = RB[(k, 2 * half + i)][:].rearrange("n u p e -> n (u p e)").bitcast(F32)
+                    for e in range(2):
+                        nc.tensor.transpose(xv[:, i, e, :], rbw[:, 128 * e : 128 * e + 128], ident[:])
+                nc.scalar.copy(out=gw[:, 2 * half : 2 * half + 2], in_=xv.rearrange("p i u n -> p i n u"))
+
+            def planes_store(k):
+                g, n0, wd, route = PLAN[k]
+                cw = sb.tile([128, 512], U32, name="cw", tag="cw", bufs=2, align_bytes=64)
+                cs = sb.tile([128, 512], U8, name="cs", tag="cs", bufs=2, align_bytes=64)
+                quantize(cw[:, :wd], cs[:, :wd], GR[k][:, :wd, :])
+                nc.sync.dma_start(out=out_words[g].rearrange("p m t -> p (m t)").bitcast(I32)[:, n0 : n0 + wd], in_=cw[:, :wd].bitcast(I32))
+                for q in range(4):
+                    nc.sync.dma_start(
+                        out=out_scales[g, 4 * q : 4 * q + 4, :].bitcast(I32)[:, n0 // 4 : n0 // 4 + wd // 4],
+                        in_=cs[32 * q : 32 * q + 4, :wd].bitcast(I32),
+                    )
+
+            prep_u(0, "vs")
+            prep_w(0, "v")
+            prep_w(1, "v")
+            for p in range(NP):
+                copy("g", a_bc[:, p, :], a_raw[:, :, p])
+            for t in range(4):
+                open_x(0, t)
+            for p in range(NP):
+                prep_q(p, 0, "ssss")
+                prep_v(p, 0, "ss")
+                if p + 2 < NP:
+                    prep_w(p + 2, "v")
+                for t in range(4):
+                    products(0, t, p)
+                    if p > 0:
+                        argument(0, t, p - 1)
+            prep_u(1, "ss")
+            for t in range(4):
+                argument(0, t, 3)
+            for t in range(4):
+                prep_q(t, 1, "ssss")
+            for t in range(4):
+                prep_v(t, 1, "ss")
+        pool_of["late"] = ctx.enter_context(tc.tile_pool(name="late", bufs=1))
+
+        def logs(k):
+            for j in range(PLAN[k][2] // 128):
+                recip_a(k, j)
+
+        def recips(k):
+            for j in range(PLAN[k][2] // 128):
+                recip_b(k, j)
+
+        EAGER = (-1,)
+        LPOS = [9, 4, 4, 4, -1]
+        last = len(PLAN)
+        mixes = []
+
+        def queue_mixes(k):
+            def both(h):
+                mix(k - 1, 2 * h)
+                mix(k - 1, 2 * h + 1)
+                planes_turn(k - 1, h)
+
+            for h in range(PLAN[k - 1][2] // 256):
+                mixes.append(lambda h=h: both(h))
+            mixes.append(lambda: planes_store(k - 1))
+        for k in range(last + 1):
+            fills = []
+
+            def fill(n):
+                for _ in range(n):
+                    if fills:
+                        fills.pop(0)()
+
+            if k == last:
+                for m in mixes:
+                    m()
+                mixes = []
+            if k > 0:
+                for t in range(4):
+                    expo(k - 1, t)
+                for t in range(4):
+                    for p in range(NP):
+                        fills.append(lambda t=t, p=p: weigh(k - 1, t, p))
+                if LPOS[k] == -1:
+                    logs(k - 1)
+                    recips(k - 1)
+            if 0 < k < last and PLAN[k][3] == "t":
+                for t in range(4):
+                    open_x(k, t)
+            if k < last:
+                nc_ = cells(k)
+                for i in range(nc_):
+                    if k > 0:
+                        if PLAN[k][3] == "d":
+                            open_x(k, i)
+                        for p in range(NP):
+                            products(k, i, p)
+                        for p in range(NP):
+                            argument(k, i, p)
+                            if i >= 3:
+                                fill(1)
+                    max_a(k, i)
+                    max_b(k, i)
+                    if i >= 0:
+                        fill(0)
+                    shift_silu(k, i)
+                    if LPOS[k] == i:
+                        logs(k - 1)
+                        recips(k - 1)
+                    if mixes:
+                        mixes.pop(0)()
+            if k > 0:
+                fill(16)
+                if LPOS[k] == 4:
+                    logs(k - 1)
+                    recips(k - 1)
+                queue_mixes(k)
+                if LPOS[k] in EAGER:
+                    for m in mixes:
+                        m()
+                    mixes = []
+                if k == last:
+                    for m in mixes:
+                        m()

@@ -19,7 +19,7 @@ D = 512
 K = 512
 FLOPS = 2 * NP * N * D * K + 2 * NP * N * M * K
 WINDOW = 32.0
-VEC_SUB = {"d": 2}
+VEC_SUB = {"d": 4}
 PLAN = [(0, 0, 512, "d"), (0, 512, 512, "d"), (1, 512, 512, "d"), (1, 0, 512, "d")]
 LBUFS = {"lg": 2, "lw": 2, "s": 4, "e": 0}
 

@@ -19,7 +19,7 @@ D = 512
 K = 512
 FLOPS = 2 * NP * N * D * K + 2 * NP * N * M * K
 WINDOW = 32.0
-VEC_SUB = {"d": 4}
+C_MIN = 1e-20
 PLAN = [(0, 0, 512, "d"), (0, 512, 512, "d"), (1, 512, 512, "d"), (1, 0, 512, "d")]
 LBUFS = {"lg": 2, "lw": 2, "s": 4, "e": 0}
 
@@ -47,8 +47,6 @@ def tile_mixtureoflogitsretrievalscore_x1_kernel(tc, u, w, v, a, b, c, out, out_
             nc.scalar.dma_start(out=c_b[:], in_=c.partition_broadcast(128))
             b_b = keep.tile([128, 2, 16], BF16)
             nc.scalar.dma_start(out=b_b[:], in_=b.rearrange("(g p t) c -> p g (t c)", p=128, t=4))
-            a_b = keep.tile([128, 8, NP], BF16)
-            nc.scalar.dma_start(out=a_b[:], in_=a.rearrange("(i p) c -> p i c", p=128))
 
             raws = {}
 
@@ -69,7 +67,7 @@ def tile_mixtureoflogitsretrievalscore_x1_kernel(tc, u, w, v, a, b, c, out, out_
             load_u(0)
             load_w(0)
             load_v(0, 0)
-            a_raw = pro.tile([128, N, NP], BF16)
+            a_raw = keep.tile([128, N, NP], BF16)
             nc.sync.dma_start(out=a_raw[:].rearrange("q n p -> q (n p)"), in_=a.rearrange("n p -> (n p)").partition_broadcast(128))
             for p in range(1, NP):
                 load_w(p)
@@ -81,10 +79,18 @@ def tile_mixtureoflogitsretrievalscore_x1_kernel(tc, u, w, v, a, b, c, out, out_
 
             c_f = keep.tile([128, NP], F32)
             nc.vector.tensor_copy(out=c_f[:], in_=c_b[:])
-            b_f = keep.tile([128, 32], F32)
-            nc.vector.tensor_copy(out=b_f[:], in_=b_b[:].rearrange("p g x -> p (g x)"))
-            a_f = keep.tile([128, 32], F32)
-            nc.vector.tensor_copy(out=a_f[:], in_=a_b[:].rearrange("p g x -> p (g x)"))
+            b_f = keep.tile([128, 8, NP], F32)
+            nc.vector.tensor_copy(out=b_f[:].rearrange("p x c -> p (x c)"), in_=b_b[:].rearrange("p g x -> p (g x)"))
+            tiny = keep.tile([128, 3, NP], F32)
+            nc.vector.scalar_tensor_tensor(out=tiny[:, 0, :], in0=c_f[:], scalar=-1.0, in1=c_f[:], op0=ALU.mult, op1=ALU.max)
+            nc.vector.tensor_scalar(out=tiny[:, 1, :], in0=tiny[:, 0, :], scalar1=C_MIN, scalar2=C_MIN, op0=ALU.is_lt, op1=ALU.mult)
+            nc.vector.tensor_scalar(out=tiny[:, 2, :], in0=tiny[:, 0, :], scalar1=C_MIN, scalar2=None, op0=ALU.is_ge)
+            nc.vector.tensor_tensor(out=c_f[:], in0=c_f[:], in1=tiny[:, 2, :], op=ALU.mult)
+            nc.vector.tensor_tensor(out=c_f[:], in0=c_f[:], in1=tiny[:, 1, :], op=ALU.add)
+            rc = keep.tile([128, NP], F32)
+            nc.vector.reciprocal(out=rc[:], in_=c_f[:])
+            bc_f = keep.tile([128, 8, NP], F32)
+            nc.vector.tensor_tensor(out=bc_f[:], in0=b_f[:], in1=rc[:].unsqueeze(1).to_broadcast([128, 8, NP]), op=ALU.mult)
 
             u_q = pro.tile([128, N], U32, align_bytes=64)
             u_s = pro.tile([128, N], U8, align_bytes=64)
@@ -94,7 +100,6 @@ def tile_mixtureoflogitsretrievalscore_x1_kernel(tc, u, w, v, a, b, c, out, out_
             q_s = keep.tile([128, NP, N], U8, align_bytes=64)
             v_q = keep.tile([128, NP, M], U32, align_bytes=64)
             v_s = keep.tile([128, NP, M], U8, align_bytes=64)
-            a_bc = keep.tile([128, NP, N], BF16)
 
             def grp_tile(pool):
                 t = pool.tile([128, 512, 4], BF16, name="grp", tag="grp", bufs=4 if pool is pro else 2, align_bytes=64)
@@ -189,89 +194,60 @@ def tile_mixtureoflogitsretrievalscore_x1_kernel(tc, u, w, v, a, b, c, out, out_
                     stop=True,
                 )
 
-            def open_x(k, t):
-                if k % 3 == 2:
+            G0 = []
+            for g, n0, wd, route in PLAN:
+                G0.append(sum(1 if r[3] == "d" else 2 for r in PLAN[: len(G0)]))
+
+            def group_tile(idx):
+                if idx % 3 == 2:
                     x = pool_of["late"].tile([128, NP, 512], F32, name="xb", tag="xb", bufs=4)
                 else:
-                    x = sb.tile([128, NP, 512], F32, name="x", tag="x", bufs=8)
-                X[(k, t)] = x
+                    x = sb.tile([128, NP, 512], F32, name="x", tag="x%d" % (idx % 3), bufs=4)
+                return x
 
-            def cells(k):
-                g, n0, wd, route = PLAN[k]
-                return 4 if route == "d" else wd // 128
+            Y = {}
 
-            def products(k, i, p):
-                g, n0, wd, route = PLAN[k]
-                ab = sb.tile([128, 512], F32, name="ab", tag="ab", bufs=6)
-                if route == "d":
-                    col = 16 * g + 4 * i + p
-                    src, sc, width = a_bc[:, p, n0 : n0 + wd], b_f[:, col : col + 1], wd
-                else:
-                    src, sc, width = None, None, 512
-                AB[(k, i, p)] = ab
-                nc.gpsimd.tensor_scalar(out=ab[:, :width], in0=src, scalar1=sc, scalar2=-WINDOW, op0=ALU.mult, op1=ALU.add)
+            def width(k):
+                return PLAN[k][2] if PLAN[k][3] == "d" else 512
 
-            def cell_of(k, i):
-                g, n0, wd, route = PLAN[k]
-                if route == "d":
-                    return X[(k, i)][:, :, :wd]
-                if (k, i) not in C:
-                    xn = sb.tile([128, NP, 512], F32, name="xn", tag="xn", bufs=2)
-                    C[(k, i)] = xn
-                return C[(k, i)][:]
+            def ncells(k):
+                return 4 if PLAN[k][3] == "d" else PLAN[k][2] // 128
+
+            def open_y(k, i):
+                Y[(k, i)] = group_tile(G0[k])
+                if PLAN[k][3] == "d":
+                    X[(k, i)] = Y[(k, i)]
 
             def argument(k, i, p):
                 g, n0, wd, route = PLAN[k]
                 acc = bank("lg")
+                y = Y[(k, i)][:, p, : width(k)]
                 if route == "d":
-                    width = wd
                     mx(acc[:, :wd], v_q, v_s, 512 * g + 128 * i, q_q, q_s, n0, wd, p)
-                else:
-                    width = 512
-                    mx(acc[:], q_q, q_s, n0 + 128 * i, v_q, v_s, 512 * g, 512, p)
-                nc.vector.scalar_tensor_tensor(
-                    out=cell_of(k, i)[:, p, :], in0=acc[:, :width], scalar=c_f[:, p : p + 1], in1=AB[(k, i, p)][:, :width], op0=ALU.mult, op1=ALU.add
-                )
+                    free, part = a_raw[:, n0 : n0 + wd, p], bc_f[:, 4 * g + i, p : p + 1]
+                nc.vector.scalar_tensor_tensor(out=y, in0=free, scalar=part, in1=acc[:, : width(k)], op0=ALU.mult, op1=ALU.add)
+
+            def silu(k, i, p):
+                y = Y[(k, i)][:, p, : width(k)]
+                nc.scalar.activation(out=y, in_=y, func=ACT.Silu, scale=c_f[:, p : p + 1])
 
             def max_a(k, i):
-                x = cell_of(k, i)
-                wd = PLAN[k][2] if PLAN[k][3] == "d" else 512
-                m2 = sb.tile([128, 2, 512], F32, name="m2", tag="m2", bufs=1)
+                y = Y[(k, i)]
+                wd = width(k)
+                m2 = sb.tile([128, 2, 512], F32, name="m2", tag="m2", bufs=2)
                 M2[(k, i)] = m2
-                nc.vector.tensor_tensor(out=m2[:, :, :wd], in0=x[:, 0:2, :], in1=x[:, 2:4, :], op=ALU.max)
+                nc.vector.tensor_tensor(out=m2[:, :, :wd], in0=y[:, 0:2, :wd], in1=y[:, 2:4, :wd], op=ALU.max)
 
             def max_b(k, i):
                 m2 = M2[(k, i)]
-                wd = PLAN[k][2] if PLAN[k][3] == "d" else 512
-                s = sb.tile([128, 512], F32, name="s", tag="shift", bufs=2)
+                wd = width(k)
+                s = sb.tile([128, 512], F32, name="s", tag="shift", bufs=3)
                 SH[(k, i)] = s
-                nc.vector.scalar_tensor_tensor(out=s[:, :wd], in0=m2[:, 0, :wd], scalar=0.0, in1=m2[:, 1, :wd], op0=ALU.max, op1=ALU.max)
-                if PLAN[k][3] != "d":
-                    nc.vector.tensor_scalar(out=s[:], in0=s[:], scalar1=-1.0, scalar2=0.0, op0=ALU.mult, op1=ALU.add)
+                nc.vector.tensor_tensor(out=s[:, :wd], in0=m2[:, 0, :wd], in1=m2[:, 1, :wd], op=ALU.max)
 
-            def shift_silu(k, i):
-                g, n0, wd, route = PLAN[k]
-                x = cell_of(k, i)
-                if route == "d":
-                    for p in range(NP):
-                        eng = nc.vector if p < VEC_SUB["d"] else nc.gpsimd
-                        eng.tensor_tensor(out=x[:, p, :], in0=x[:, p, :], in1=SH[(k, i)][:, :wd], op=ALU.subtract)
-                    nc.scalar.activation(out=x, in_=x, func=ACT.Silu, bias=window[:], scale=1.0)
-                else:
-                    for t in range(4):
-                        acc = bank("e")
-                        blk = slice(128 * t, 128 * t + 128)
-                        for p in range(NP):
-                            quarter = acc[:, 128 * p : 128 * p + 128]
-                            nc.tensor.matmul(out=quarter, lhsT=x[:, p, blk], rhs=ident[:], is_transpose=True, start=True, stop=False)
-                            nc.tensor.matmul(out=quarter, lhsT=SH[(k, i)][:, blk], rhs=ident[:], is_transpose=True, start=False, stop=True)
-                        nc.scalar.activation(
-                            out=X[(k, t)][:, :, 128 * i : 128 * i + 128],
-                            in_=acc[:].rearrange("m (p n) -> m p n", p=NP),
-                            func=ACT.Silu,
-                            bias=window[:],
-                            scale=1.0,
-                        )
+            def shift(k, i, p):
+                y = Y[(k, i)][:, p, : width(k)]
+                nc.vector.tensor_tensor(out=y, in0=y, in1=SH[(k, i)][:, : width(k)], op=ALU.subtract)
 
             def expo(k, t):
                 x = X[(k, t)][:, :, : PLAN[k][2]]
@@ -355,23 +331,24 @@ def tile_mixtureoflogitsretrievalscore_x1_kernel(tc, u, w, v, a, b, c, out, out_
             prep_u(0, "vs")
             prep_w(0, "v")
             prep_w(1, "v")
-            for p in range(NP):
-                copy("g", a_bc[:, p, :], a_raw[:, :, p])
             for t in range(4):
-                open_x(0, t)
+                open_y(0, t)
             for p in range(NP):
                 prep_q(p, 0, "ssss")
                 prep_v(p, 0, "ss")
                 if p + 2 < NP:
                     prep_w(p + 2, "v")
-                for t in range(4):
-                    products(0, t, p)
-                    if p > 0:
+                if p > 0:
+                    for t in range(4):
                         argument(0, t, p - 1)
+
             prep_u(1, "ss")
             for t in range(4):
                 argument(0, t, 3)
+
             for t in range(4):
+                for p in range(NP):
+                    silu(0, t, p)
                 prep_q(t, 1, "ssss")
             for t in range(4):
                 prep_v(t, 1, "ss")
@@ -380,81 +357,88 @@ def tile_mixtureoflogitsretrievalscore_x1_kernel(tc, u, w, v, a, b, c, out, out_
         def logs(k):
             for j in range(PLAN[k][2] // 128):
                 recip_a(k, j)
-
-        def recips(k):
             for j in range(PLAN[k][2] // 128):
                 recip_b(k, j)
 
-        EAGER = (-1,)
-        LPOS = [9, 4, 4, 4, -1]
-        last = len(PLAN)
-        mixes = []
+        cells = [(k, i) for k in range(len(PLAN)) for i in range(ncells(k))]
+        fills = []
+
+        def fill(n):
+            for _ in range(n):
+                if fills:
+                    fills.pop(0)()
 
         def queue_mixes(k):
-            def both(h):
-                mix(k - 1, 2 * h)
-                mix(k - 1, 2 * h + 1)
-                planes_turn(k - 1, h)
+            nj = PLAN[k][2] // 128
+            for j in range(nj):
+                fills.append(lambda j=j: mix(k, j))
+                if j == nj - 1 or j % 2 == 1:
+                    fills.append(lambda j=j: planes_turn(k, j // 2))
+            fills.append(lambda: planes_store(k))
 
-            for h in range(PLAN[k - 1][2] // 256):
-                mixes.append(lambda h=h: both(h))
-            mixes.append(lambda: planes_store(k - 1))
-        for k in range(last + 1):
-            fills = []
+        def queue_weigh(k):
+            for t in range(4):
+                for p in range(NP):
+                    fills.append(lambda t=t, p=p: weigh(k, t, p))
 
-            def fill(n):
-                for _ in range(n):
-                    if fills:
-                        fills.pop(0)()
+        LATE = [9, 4, 4, 4]
+        FL = [(0, 0), (4, 2), (4, 2), (4, 2)]
 
-            if k == last:
-                for m in mixes:
-                    m()
-                mixes = []
-            if k > 0:
-                for t in range(4):
-                    expo(k - 1, t)
-                for t in range(4):
-                    for p in range(NP):
-                        fills.append(lambda t=t, p=p: weigh(k - 1, t, p))
-                if LPOS[k] == -1:
-                    logs(k - 1)
-                    recips(k - 1)
-            if 0 < k < last and PLAN[k][3] == "t":
-                for t in range(4):
-                    open_x(k, t)
-            if k < last:
-                nc_ = cells(k)
-                for i in range(nc_):
-                    if k > 0:
-                        if PLAN[k][3] == "d":
-                            open_x(k, i)
-                        for p in range(NP):
-                            products(k, i, p)
-                        for p in range(NP):
-                            argument(k, i, p)
-                            if i >= 3:
-                                fill(1)
-                    max_a(k, i)
-                    max_b(k, i)
-                    if i >= 0:
-                        fill(0)
-                    shift_silu(k, i)
-                    if LPOS[k] == i:
-                        logs(k - 1)
-                        recips(k - 1)
-                    if mixes:
-                        mixes.pop(0)()
-            if k > 0:
-                fill(16)
-                if LPOS[k] == 4:
-                    logs(k - 1)
-                    recips(k - 1)
-                queue_mixes(k)
-                if LPOS[k] in EAGER:
-                    for m in mixes:
-                        m()
-                    mixes = []
-                if k == last:
-                    for m in mixes:
-                        m()
+        early = set()
+
+        def args(k, i, n):
+            open_y(k, i)
+            early.add((k, i))
+            for p in range(NP):
+                argument(k, i, p)
+                if p >= NP - n:
+                    fill(1)
+
+        def head(k, i, n):
+            if (k, i) not in early:
+                args(k, i, n)
+            else:
+                fill(n)
+            for p in range(NP):
+                silu(k, i, p)
+
+        def rest(k, i, n):
+            max_a(k, i)
+            fill(1 if n > 0 else 0)
+            max_b(k, i)
+            fill(1 if n > 1 else 0)
+            if PLAN[k][3] == "d":
+                for p in range(NP):
+                    shift(k, i, p)
+
+        for s, (k, i) in enumerate(cells):
+            f = FL[i * 4 // ncells(k)] if k > 0 else (0, 0)
+            nxt = cells[s + 1] if s + 1 < len(cells) else None
+            lastc = i == ncells(k) - 1
+            if lastc and k > 0 and LATE[k] == 4:
+                fill(99)
+                logs(k - 1)
+                queue_mixes(k - 1)
+            if nxt and nxt[0] > 0 and not lastc:
+                head(nxt[0], nxt[1], f[0])
+            rest(k, i, f[1])
+            if k > 0 and i == LATE[k]:
+                logs(k - 1)
+            if lastc:
+                if k > 0 and LATE[k] != 4:
+                    fill(99)
+                    queue_mixes(k - 1)
+                for c in cells[s + 1 : s + 1 + (1 if PLAN[k][3] == "d" else 2)]:
+                    if c[0] == k + 1:
+                        args(c[0], c[1], 0)
+                if PLAN[k][3] == "d":
+                    for t in range(4):
+                        expo(k, t)
+                if nxt:
+                    head(nxt[0], nxt[1], 0)
+
+                queue_weigh(k)
+        fill(99)
+        logs(len(PLAN) - 1)
+        queue_mixes(len(PLAN) - 1)
+        fill(99)

@@ -17,11 +17,10 @@ N = 1024
 M = 1024
 D = 512
 K = 512
-FLOPS = 2 * NP * N * D * K + 2 * NP * N * M * K
-WINDOW = 32.0
 C_MIN = 1e-20
-PLAN = [(0, 0, 512, "d"), (0, 512, 512, "d"), (1, 512, 512, "d"), (1, 0, 512, "d")]
-LBUFS = {"lg": 2, "lw": 2, "s": 4, "e": 0}
+FLOPS = 2 * NP * N * D * K + 2 * NP * N * M * K
+
+BATCHES = ((0, 0), (0, 512), (1, 512), (1, 0))
 
 
 def tile_mixtureoflogitsretrievalscore_x1_kernel(tc, u, w, v, a, b, c, out, out_words, out_scales):
@@ -29,31 +28,249 @@ def tile_mixtureoflogitsretrievalscore_x1_kernel(tc, u, w, v, a, b, c, out, out_
     with ExitStack() as ctx:
         keep = ctx.enter_context(tc.tile_pool(name="keep", bufs=1))
         sb = ctx.enter_context(tc.tile_pool(name="sb", bufs=2))
-        ps = ctx.enter_context(tc.psum_pool(name="ps", bufs=2))
-        with tc.tile_pool(name="pro", bufs=1) as pro:
-            ctx.enter_context(tc.manual_schedule(engines={mybir.EngineType.Activation}))
-            pool_of = {}
+        ps = ctx.enter_context(tc.psum_pool(name="ps", bufs=5))
+        ctx.enter_context(tc.manual_schedule())
 
-            def bank(tag):
-                t = ps.tile([128, 512], F32, name=tag, tag=tag, bufs=LBUFS[tag])
-                return t
+        def logit_bank():
+            acc = ps.tile([128, 512], F32, name="logit", tag="logit", bufs=5)
+            return acc
 
-            ident = keep.tile([128, 128], F32)
-            make_identity(nc, ident[:])
-            window = keep.tile([128, 1], F32)
-            nc.gpsimd.memset(window[:], WINDOW)
+        def other_bank():
+            acc = ps.tile([128, 512], F32, name="other", tag="other", bufs=3)
+            return acc
 
-            c_b = keep.tile([128, NP], BF16)
-            nc.scalar.dma_start(out=c_b[:], in_=c.partition_broadcast(128))
-            b_b = keep.tile([128, 2, 16], BF16)
-            nc.scalar.dma_start(out=b_b[:], in_=b.rearrange("(g p t) c -> p g (t c)", p=128, t=4))
+        ident = keep.tile([128, 128], F32)
+        make_identity(nc, ident[:])
 
+        c_b = keep.tile([128, NP], BF16)
+        nc.scalar.dma_start(out=c_b[:], in_=c.partition_broadcast(128))
+        b_b = keep.tile([128, 2, 4 * NP], BF16)
+        nc.scalar.dma_start(out=b_b[:], in_=b.rearrange("(g p t) c -> p g (t c)", p=128, t=4))
+        a_all = keep.tile([128, N, NP], BF16)
+
+        q_q = keep.tile([128, NP, N], U32, align_bytes=64)
+        q_s = keep.tile([128, NP, N], U8, align_bytes=64)
+        v_q = keep.tile([128, NP, M], U32, align_bytes=64)
+        v_s = keep.tile([128, NP, M], U8, align_bytes=64)
+
+        def load_a():
+            nc.sync.dma_start(out=a_all[:].rearrange("q n c -> q (n c)"), in_=a.rearrange("n c -> (n c)").partition_broadcast(128))
+
+        c_f = keep.tile([128, NP], F32)
+        nc.vector.tensor_copy(out=c_f[:], in_=c_b[:])
+        b_f = keep.tile([128, 8, NP], F32)
+        nc.vector.tensor_copy(out=b_f[:].rearrange("p x c -> p (x c)"), in_=b_b[:].rearrange("p g x -> p (g x)"))
+        c_abs = keep.tile([128, NP], F32)
+        nc.vector.scalar_tensor_tensor(out=c_abs[:], in0=c_f[:], scalar=-1.0, in1=c_f[:], op0=ALU.mult, op1=ALU.max)
+        c_fill = keep.tile([128, NP], F32)
+        nc.vector.tensor_scalar(out=c_fill[:], in0=c_abs[:], scalar1=C_MIN, scalar2=C_MIN, op0=ALU.is_lt, op1=ALU.mult)
+        c_big = keep.tile([128, NP], F32)
+        nc.vector.tensor_scalar(out=c_big[:], in0=c_abs[:], scalar1=C_MIN, scalar2=None, op0=ALU.is_ge)
+        nc.vector.tensor_tensor(out=c_f[:], in0=c_f[:], in1=c_big[:], op=ALU.mult)
+        nc.vector.tensor_tensor(out=c_f[:], in0=c_f[:], in1=c_fill[:], op=ALU.add)
+        c_inv = keep.tile([128, NP], F32)
+        nc.vector.reciprocal(out=c_inv[:], in_=c_f[:])
+        b_over_c = keep.tile([128, 8, NP], F32)
+        nc.vector.tensor_tensor(out=b_over_c[:], in0=b_f[:], in1=c_inv[:].unsqueeze(1).to_broadcast([128, 8, NP]), op=ALU.mult)
+
+        def quantize(codes, scales, grouped):
+            nc.vector.quantize_mx(out=codes.bitcast(FP8X4), scales=scales, in_=grouped[:].rearrange("p n f -> p (n f)"))
+
+        def as_words(grouped):
+            return grouped[:].rearrange("p n f -> p (n f)").bitcast(F32).rearrange("p (i n e) -> p i n e", n=128, e=2)
+
+        def copy(engine, dst, src):
+            if engine == "v":
+                nc.vector.tensor_copy(out=dst, in_=src)
+            elif engine == "s":
+                nc.scalar.copy(out=dst, in_=src)
+            else:
+                nc.gpsimd.tensor_scalar(out=dst, in0=src, scalar1=1.0, scalar2=0.0, op0=ALU.mult, op1=ALU.add)
+
+        Y, E, EL, SH, ZS, RZ, RB, GR = {}, {}, {}, {}, {}, {}, {}, {}
+        late = []
+
+        def mx_logits(k, t, p):
+            g, n0 = BATCHES[k]
+            m0 = 512 * g + 128 * t
+            acc = logit_bank()
+            nc.tensor.matmul_mx(
+                out=acc[:],
+                lhsT=v_q[:, p, m0 : m0 + 128].bitcast(FP8X4),
+                lhsT_scale=v_s[:, p, m0 : m0 + 128],
+                rhs=q_q[:, p, n0 : n0 + 512].bitcast(FP8X4),
+                rhs_scale=q_s[:, p, n0 : n0 + 512],
+                start=True,
+                stop=True,
+            )
+            return acc
+
+        def open_cell(k, t):
+            if k == 2:
+                y = late[0].tile([128, NP, 512], F32, name="y2", tag="y2", bufs=4)
+            else:
+                y = sb.tile([128, NP, 512], F32, name="y", tag="y%d" % (k % 3), bufs=4)
+            Y[k, t] = y
+
+        def argument(k, t, p):
+            g, n0 = BATCHES[k]
+            acc = mx_logits(k, t, p)
+            nc.vector.scalar_tensor_tensor(
+                out=Y[k, t][:, p, :], in0=a_all[:, n0 : n0 + 512, p], scalar=b_over_c[:, 4 * g + t, p : p + 1], in1=acc[:], op0=ALU.mult, op1=ALU.add
+            )
+
+        def silu(k, t):
+            for p in range(NP):
+                y = Y[k, t][:, p, :]
+                nc.scalar.activation(out=y, in_=y, func=ACT.Silu, scale=c_f[:, p : p + 1])
+
+        def max_pairs(k, t):
+            y = Y[k, t]
+            m2 = sb.tile([128, 2, 512], F32, name="m2", tag="m2", bufs=1)
+            nc.vector.tensor_tensor(out=m2[:], in0=y[:, 0:2, :], in1=y[:, 2:4, :], op=ALU.max)
+            SH[k, t] = m2
+
+        def max_all(k, t):
+            m2 = SH[k, t]
+            s = sb.tile([128, 512], F32, name="s", tag="s", bufs=3)
+            nc.vector.tensor_tensor(out=s[:], in0=m2[:, 0, :], in1=m2[:, 1, :], op=ALU.max)
+            SH[k, t] = s
+
+        def shift(k, t):
+            for p in range(NP):
+                engine = nc.gpsimd if t in (3,) else nc.vector
+                y = Y[k, t][:, p, :]
+                engine.tensor_tensor(out=y, in0=y, in1=SH[k, t][:], op=ALU.subtract)
+
+        def expo(k, t):
+            nc.scalar.activation(out=Y[k, t][:], in_=Y[k, t][:], func=ACT.Exp)
+
+        def weigh(k, t):
+            el = sb.tile([128, NP, 512], F32, name="el", tag="el", bufs=4)
+            EL[k, t] = el
+            for p in range(NP):
+                acc = mx_logits(k, t, p)
+                nc.vector.tensor_tensor(out=el[:, p, :], in0=acc[:], in1=Y[k, t][:, p, :], op=ALU.mult)
+
+        def sum_components(cells, k, j):
+            acc = other_bank()
+            for t in range(4):
+                for p in range(NP):
+                    nc.tensor.matmul(
+                        out=acc[:, 128 * t : 128 * t + 128],
+                        lhsT=cells[k, t][:, p, 128 * j : 128 * j + 128],
+                        rhs=ident[:],
+                        is_transpose=True,
+                        start=(p == 0),
+                        stop=(p == NP - 1),
+                    )
+            return acc
+
+        def z_sum(k, j):
+            ZS[k, j] = sum_components(Y, k, j)
+
+        def reciprocals(k):
+            for j in range(4):
+                if (k, j) not in ZS:
+                    z_sum(k, j)
+                rz = sb.tile([128, 512], F32, name="rz", tag="rz", bufs=4)
+                RZ[k, j] = rz
+                nc.scalar.activation(out=rz[:].rearrange("n (p t) -> n p t", t=4), in_=ZS[k, j][:].rearrange("n (t p) -> n p t", t=4), func=ACT.Ln)
+            for j in range(4):
+                nc.scalar.activation(out=RZ[k, j][:], in_=RZ[k, j][:], func=ACT.Exp, scale=-1.0)
+
+        def mix(k, j):
+            g, n0 = BATCHES[k]
+            num = sum_components(EL, k, j)
+            r = sb.tile([128, 512], F32, name="r", tag="r", bufs=2)
+            nc.vector.tensor_tensor(
+                out=r[:].rearrange("n (p t) -> n p t", t=4),
+                in0=num[:].rearrange("n (t p) -> n p t", t=4),
+                in1=RZ[k, j][:].rearrange("n (p t) -> n p t", t=4),
+                op=ALU.mult,
+            )
+            n1 = n0 + 128 * j
+            nc.sync.dma_start(out=out[n1 : n1 + 128, 512 * g : 512 * g + 512], in_=r[:])
+            rb = sb.tile([128, 2, 128, 2], BF16, name="rb", tag="rb", bufs=4)
+            RB[k, j] = rb
+            copy("g", rb[:], r[:].rearrange("n (p e f) -> n e p f", e=2, f=2))
+
+        def planes_turn(k, half):
+            if half == 0:
+                grouped = sb.tile([128, 512, 4], BF16, name="planes", tag="planes", bufs=2, align_bytes=64)
+                GR[k] = grouped
+            bank = other_bank()
+            view = bank[:].rearrange("p (i e n) -> p i e n", i=2, e=2)
+            for i in range(2):
+                words = RB[k, 2 * half + i][:].rearrange("n e p f -> n (e p f)").bitcast(F32)
+                for e in range(2):
+                    nc.tensor.transpose(view[:, i, e, :], words[:, 128 * e : 128 * e + 128], ident[:])
+            nc.scalar.copy(out=as_words(GR[k])[:, 2 * half : 2 * half + 2], in_=view.rearrange("p i e n -> p i n e"))
+
+        def planes_store(k):
+            g, n0 = BATCHES[k]
+            codes = sb.tile([128, 512], U32, name="codes", tag="codes", bufs=2, align_bytes=64)
+            scales = sb.tile([128, 512], U8, name="scales", tag="scales", bufs=2, align_bytes=64)
+            quantize(codes[:], scales[:], GR[k])
+            nc.sync.dma_start(out=out_words[g].rearrange("p m t -> p (m t)").bitcast(I32)[:, n0 : n0 + 512], in_=codes[:].bitcast(I32))
+            for q in range(4):
+                nc.sync.dma_start(
+                    out=out_scales[g, 4 * q : 4 * q + 4, :].bitcast(I32)[:, n0 // 4 : n0 // 4 + 128],
+                    in_=scales[32 * q : 32 * q + 4, :].bitcast(I32),
+                )
+
+        last = len(BATCHES) - 1
+
+        def shift_phase(k, front):
+            todo = []
+            for t in range(4):
+                if k > 0 and t == 2:
+                    todo = [0, 1, 2, 3]
+                max_pairs(k, t)
+                if todo:
+                    mix(k - 1, todo.pop(0))
+                max_all(k, t)
+                if todo:
+                    mix(k - 1, todo.pop(0))
+                shift(k, t)
+                for f in front[t]:
+                    f()
+            for j in todo:
+                mix(k - 1, j)
+
+        def weigh_phase(k):
+            for t in range(4):
+                expo(k, t)
+            for t in range(4):
+                if k < last:
+                    open_cell(k + 1, t)
+                    for p in range(NP):
+                        argument(k + 1, t, p)
+                if k > 0 and t == 1:
+                    planes_turn(k - 1, 0)
+                    planes_turn(k - 1, 1)
+                if k > 0 and t == 3:
+                    planes_store(k - 1)
+                if t == 3:
+                    if k == last:
+                        reciprocals(k)
+                    else:
+                        z_sum(k, 0)
+                weigh(k, t)
+            if k < last:
+                for j in (1, 2):
+                    z_sum(k, j)
+                for t in range(4):
+                    silu(k + 1, t)
+                reciprocals(k)
+
+        with tc.tile_pool(name="front", bufs=1) as fr:
             raws = {}
 
             def load(key, src):
-                t = pro.tile([128, 4, 512], BF16, name="raw", tag="raw", bufs=5)
-                nc.sync.dma_start(out=t[:], in_=src)
-                raws[key] = t
+                raw = fr.tile([128, 4, 512], BF16, name="raw", tag="raw", bufs=5)
+                nc.sync.dma_start(out=raw[:], in_=src)
+                raws[key] = raw
 
             def load_u(h):
                 load(("u", h), u[512 * h : 512 * h + 512, :].rearrange("(i p) d -> p i d", p=128))
@@ -67,98 +284,60 @@ def tile_mixtureoflogitsretrievalscore_x1_kernel(tc, u, w, v, a, b, c, out, out_
             load_u(0)
             load_w(0)
             load_v(0, 0)
-            a_raw = keep.tile([128, N, NP], BF16)
-            nc.sync.dma_start(out=a_raw[:].rearrange("q n p -> q (n p)"), in_=a.rearrange("n p -> (n p)").partition_broadcast(128))
-            for p in range(1, NP):
-                load_w(p)
-                load_v(p, 0)
-                if p == 1:
-                    load_u(1)
+            load_w(1)
+            load_v(1, 0)
+            load_w(2)
+            load_a()
+            load_v(2, 0)
+            load_w(3)
+            load_v(3, 0)
+            load_u(1)
             for p in range(NP):
                 load_v(p, 1)
 
-            c_f = keep.tile([128, NP], F32)
-            nc.vector.tensor_copy(out=c_f[:], in_=c_b[:])
-            b_f = keep.tile([128, 8, NP], F32)
-            nc.vector.tensor_copy(out=b_f[:].rearrange("p x c -> p (x c)"), in_=b_b[:].rearrange("p g x -> p (g x)"))
-            tiny = keep.tile([128, 3, NP], F32)
-            nc.vector.scalar_tensor_tensor(out=tiny[:, 0, :], in0=c_f[:], scalar=-1.0, in1=c_f[:], op0=ALU.mult, op1=ALU.max)
-            nc.vector.tensor_scalar(out=tiny[:, 1, :], in0=tiny[:, 0, :], scalar1=C_MIN, scalar2=C_MIN, op0=ALU.is_lt, op1=ALU.mult)
-            nc.vector.tensor_scalar(out=tiny[:, 2, :], in0=tiny[:, 0, :], scalar1=C_MIN, scalar2=None, op0=ALU.is_ge)
-            nc.vector.tensor_tensor(out=c_f[:], in0=c_f[:], in1=tiny[:, 2, :], op=ALU.mult)
-            nc.vector.tensor_tensor(out=c_f[:], in0=c_f[:], in1=tiny[:, 1, :], op=ALU.add)
-            rc = keep.tile([128, NP], F32)
-            nc.vector.reciprocal(out=rc[:], in_=c_f[:])
-            bc_f = keep.tile([128, 8, NP], F32)
-            nc.vector.tensor_tensor(out=bc_f[:], in0=b_f[:], in1=rc[:].unsqueeze(1).to_broadcast([128, 8, NP]), op=ALU.mult)
+            u_q = fr.tile([128, N], U32, align_bytes=64)
+            u_s = fr.tile([128, N], U8, align_bytes=64)
+            w_q = fr.tile([128, NP, K], U32, align_bytes=64)
+            w_s = fr.tile([128, NP, K], U8, align_bytes=64)
 
-            u_q = pro.tile([128, N], U32, align_bytes=64)
-            u_s = pro.tile([128, N], U8, align_bytes=64)
-            w_q = pro.tile([128, NP, K], U32, align_bytes=64)
-            w_s = pro.tile([128, NP, K], U8, align_bytes=64)
-            q_q = keep.tile([128, NP, N], U32, align_bytes=64)
-            q_s = keep.tile([128, NP, N], U8, align_bytes=64)
-            v_q = keep.tile([128, NP, M], U32, align_bytes=64)
-            v_s = keep.tile([128, NP, M], U8, align_bytes=64)
+            def front_group():
+                grouped = fr.tile([128, 512, 4], BF16, name="grouped", tag="grouped", bufs=4, align_bytes=64)
+                return grouped
 
-            def grp_tile(pool):
-                t = pool.tile([128, 512, 4], BF16, name="grp", tag="grp", bufs=4 if pool is pro else 2, align_bytes=64)
-                return t
-
-            def words_of(grp):
-                return grp[:].rearrange("p n f -> p (n f)").bitcast(F32).rearrange("p (i n u) -> p i n u", n=128, u=2)
-
-            def copy(eng, dst, src):
-                if eng == "g":
-                    nc.gpsimd.tensor_scalar(out=dst, in0=src, scalar1=1.0, scalar2=0.0, op0=ALU.mult, op1=ALU.add)
-                elif eng == "v":
-                    nc.vector.tensor_copy(out=dst, in_=src)
-                else:
-                    nc.scalar.copy(out=dst, in_=src)
-
-            def quantize(codes, scales, grp):
-                nc.vector.quantize_mx(out=codes.bitcast(FP8X4), scales=scales, in_=grp.rearrange("p n f -> p (n f)"))
-
-            tags = ["s"]
-
-            def next_tag():
-                tags.append(tags.pop(0))
-                return tags[0]
-
-            def turn(raw, engs):
-                grp = grp_tile(pro)
-                rw = raw[:].rearrange("p i k -> p (i k)").bitcast(F32)
-                gw = words_of(grp)
+            def turn(raw, engine):
+                grouped = front_group()
+                words = raw[:].rearrange("p i k -> p (i k)").bitcast(F32)
                 for half in range(2):
-                    xt = bank(next_tag())
-                    xv = xt[:].rearrange("p (i u n) -> p i u n", i=2, u=2)
+                    bank = other_bank()
+                    view = bank[:].rearrange("p (i e n) -> p i e n", i=2, e=2)
                     for i in range(2):
                         for e in range(2):
                             base = 256 * (2 * half + i)
-                            nc.tensor.transpose(xv[:, i, e, :], rw[:, base + e : base + 256 : 2], ident[:])
-                    copy(engs[half], gw[:, 2 * half : 2 * half + 2], xv.rearrange("p i u n -> p i n u"))
-                return grp
+                            nc.tensor.transpose(view[:, i, e, :], words[:, base + e : base + 256 : 2], ident[:])
+                    copy(engine[half], as_words(grouped)[:, 2 * half : 2 * half + 2], view.rearrange("p i e n -> p i n e"))
+                return grouped
 
-            def prep_w(p, eng):
-                g_w = grp_tile(pro)
-                dst = g_w[:].rearrange("p x f -> p (x f)").rearrange("p (t m j) -> p t m j", t=4, j=4)
-                src = raws[("w", p)][:].rearrange("p j (m t) -> p t m j", t=4)
-                copy(eng, dst, src)
-                quantize(w_q[:, p, :], w_s[:, p, :], g_w[:])
+            def front_u(h, engine):
+                grouped = turn(raws["u", h], engine)
+                quantize(u_q[:, 512 * h : 512 * h + 512], u_s[:, 512 * h : 512 * h + 512], grouped)
 
-            def prep_u(h, engs):
-                grp = turn(raws[("u", h)], engs)
-                quantize(u_q[:, 512 * h : 512 * h + 512], u_s[:, 512 * h : 512 * h + 512], grp[:])
+            def front_w(p, engine):
+                grouped = front_group()
+                dst = grouped[:].rearrange("p x f -> p (x f)").rearrange("p (t m j) -> p t m j", t=4, j=4)
+                copy(engine, dst, raws["w", p][:].rearrange("p j (m t) -> p t m j", t=4))
+                quantize(w_q[:, p, :], w_s[:, p, :], grouped)
 
-            def prep_q(p, h, engs):
-                grp = grp_tile(pro)
-                for nb in range(4):
-                    acc = bank(next_tag())
-                    n0 = 512 * h + 128 * nb
-                    av = acc[:].rearrange("p (t n) -> p t n", t=4)
+            pending = []
+
+            def front_q(p, h, engine="ssss"):
+                grouped = front_group()
+                for i in range(4):
+                    bank = other_bank()
+                    view = bank[:].rearrange("p (t n) -> p t n", t=4)
+                    n0 = 512 * h + 128 * i
                     for t in range(4):
                         nc.tensor.matmul_mx(
-                            out=av[:, t, :],
+                            out=view[:, t, :],
                             lhsT=w_q[:, p, 128 * t : 128 * t + 128].bitcast(FP8X4),
                             lhsT_scale=w_s[:, p, 128 * t : 128 * t + 128],
                             rhs=u_q[:, n0 : n0 + 128].bitcast(FP8X4),
@@ -166,279 +345,60 @@ def tile_mixtureoflogitsretrievalscore_x1_kernel(tc, u, w, v, a, b, c, out, out_
                             start=True,
                             stop=True,
                         )
-                    copy(engs[nb], grp[:, 128 * nb : 128 * nb + 128, :], av.rearrange("p t n -> p n t"))
-                quantize(q_q[:, p, 512 * h : 512 * h + 512], q_s[:, p, 512 * h : 512 * h + 512], grp[:])
+                    copy(engine[i], grouped[:, 128 * i : 128 * i + 128, :], view.rearrange("p t n -> p n t"))
+                pending.append((q_q[:, p, 512 * h : 512 * h + 512], q_s[:, p, 512 * h : 512 * h + 512], grouped))
 
-            def prep_v(p, g, engs):
-                grp = turn(raws[("v", p, g)], engs)
-                quantize(v_q[:, p, 512 * g : 512 * g + 512], v_s[:, p, 512 * g : 512 * g + 512], grp[:])
+            def front_v(p, g, engine="ss"):
+                grouped = turn(raws["v", p, g], engine)
+                pending.append((v_q[:, p, 512 * g : 512 * g + 512], v_s[:, p, 512 * g : 512 * g + 512], grouped))
 
-            X = {}
-            EL = {}
-            AB = {}
-            C = {}
-            SH = {}
-            M2 = {}
-            RZ = {}
-            RB = {}
-            GR = {}
+            def flush(n=1):
+                for _ in range(n):
+                    quantize(*pending.pop(0))
 
-            def mx(acc, st, st_s, s0, mv, mv_s, m0, wd, p):
-                nc.tensor.matmul_mx(
-                    out=acc,
-                    lhsT=st[:, p, s0 : s0 + 128].bitcast(FP8X4),
-                    lhsT_scale=st_s[:, p, s0 : s0 + 128],
-                    rhs=mv[:, p, m0 : m0 + wd].bitcast(FP8X4),
-                    rhs_scale=mv_s[:, p, m0 : m0 + wd],
-                    start=True,
-                    stop=True,
-                )
-
-            G0 = []
-            for g, n0, wd, route in PLAN:
-                G0.append(sum(1 if r[3] == "d" else 2 for r in PLAN[: len(G0)]))
-
-            def group_tile(idx):
-                if idx % 3 == 2:
-                    x = pool_of["late"].tile([128, NP, 512], F32, name="xb", tag="xb", bufs=4)
-                else:
-                    x = sb.tile([128, NP, 512], F32, name="x", tag="x%d" % (idx % 3), bufs=4)
-                return x
-
-            Y = {}
-
-            def width(k):
-                return PLAN[k][2] if PLAN[k][3] == "d" else 512
-
-            def ncells(k):
-                return 4 if PLAN[k][3] == "d" else PLAN[k][2] // 128
-
-            def open_y(k, i):
-                Y[(k, i)] = group_tile(G0[k])
-                if PLAN[k][3] == "d":
-                    X[(k, i)] = Y[(k, i)]
-
-            def argument(k, i, p):
-                g, n0, wd, route = PLAN[k]
-                acc = bank("lg")
-                y = Y[(k, i)][:, p, : width(k)]
-                if route == "d":
-                    mx(acc[:, :wd], v_q, v_s, 512 * g + 128 * i, q_q, q_s, n0, wd, p)
-                    free, part = a_raw[:, n0 : n0 + wd, p], bc_f[:, 4 * g + i, p : p + 1]
-                nc.vector.scalar_tensor_tensor(out=y, in0=free, scalar=part, in1=acc[:, : width(k)], op0=ALU.mult, op1=ALU.add)
-
-            def silu(k, i, p):
-                y = Y[(k, i)][:, p, : width(k)]
-                nc.scalar.activation(out=y, in_=y, func=ACT.Silu, scale=c_f[:, p : p + 1])
-
-            def max_a(k, i):
-                y = Y[(k, i)]
-                wd = width(k)
-                m2 = sb.tile([128, 2, 512], F32, name="m2", tag="m2", bufs=2)
-                M2[(k, i)] = m2
-                nc.vector.tensor_tensor(out=m2[:, :, :wd], in0=y[:, 0:2, :wd], in1=y[:, 2:4, :wd], op=ALU.max)
-
-            def max_b(k, i):
-                m2 = M2[(k, i)]
-                wd = width(k)
-                s = sb.tile([128, 512], F32, name="s", tag="shift", bufs=3)
-                SH[(k, i)] = s
-                nc.vector.tensor_tensor(out=s[:, :wd], in0=m2[:, 0, :wd], in1=m2[:, 1, :wd], op=ALU.max)
-
-            def shift(k, i, p):
-                y = Y[(k, i)][:, p, : width(k)]
-                nc.vector.tensor_tensor(out=y, in0=y, in1=SH[(k, i)][:, : width(k)], op=ALU.subtract)
-
-            def expo(k, t):
-                x = X[(k, t)][:, :, : PLAN[k][2]]
-                nc.scalar.activation(out=x, in_=x, func=ACT.Exp)
-
-            def weigh(k, t, p):
-                g, n0, wd, route = PLAN[k]
-                if p == 0:
-                    el = pool_of["late"].tile([128, NP, 512], F32, name="el", tag="el", bufs=4)
-                    EL[(k, t)] = el
-                acc = bank("lw")
-                mx(acc[:, :wd], v_q, v_s, 512 * g + 128 * t, q_q, q_s, n0, wd, p)
-                nc.vector.tensor_tensor(out=EL[(k, t)][:, p, :wd], in0=acc[:, :wd], in1=X[(k, t)][:, p, :wd], op=ALU.mult)
-
-            def sum_up(x, k, j):
-                acc = bank("s")
-                for t in range(4):
-                    for p in range(NP):
-                        nc.tensor.matmul(
-                            out=acc[:, 128 * t : 128 * t + 128],
-                            lhsT=x[(k, t)][:, p, 128 * j : 128 * j + 128],
-                            rhs=ident[:],
-                            is_transpose=True,
-                            start=(p == 0),
-                            stop=(p == NP - 1),
-                        )
-                return acc
-
-            def recip_a(k, j):
-                z = sum_up(X, k, j)
-                rz = sb.tile([128, 512], F32, name="rz", tag="rz", bufs=4)
-                RZ[(k, j)] = rz
-                nc.scalar.activation(out=rz[:].rearrange("n (p t) -> n p t", t=4), in_=z[:].rearrange("n (t p) -> n p t", t=4), func=ACT.Ln)
-
-            def recip_b(k, j):
-                rz = RZ[(k, j)]
-                nc.scalar.activation(out=rz[:], in_=rz[:], func=ACT.Exp, scale=-1.0)
-
-            def mix(k, j):
-                g, nn, wd, route = PLAN[k]
-                num = sum_up(EL, k, j)
-                r = sb.tile([128, 512], F32, name="r", tag="r", bufs=2)
-                nc.vector.tensor_tensor(
-                    out=r[:].rearrange("n (p t) -> n p t", t=4),
-                    in0=num[:].rearrange("n (t p) -> n p t", t=4),
-                    in1=RZ[(k, j)][:].rearrange("n (p t) -> n p t", t=4),
-                    op=ALU.mult,
-                )
-                n0 = nn + 128 * j
-                nc.sync.dma_start(out=out[n0 : n0 + 128, 512 * g : 512 * g + 512], in_=r[:])
-                rb = sb.tile([128, 2, 128, 2], BF16, name="rb", tag="rb", bufs=2)
-                RB[(k, j)] = rb
-                nc.gpsimd.tensor_scalar(
-                    out=rb[:], in0=r[:].rearrange("n (p u e) -> n u p e", u=2, e=2), scalar1=1.0, scalar2=0.0, op0=ALU.mult, op1=ALU.add
-                )
-
-            def planes_turn(k, half):
-                if half == 0:
-                    GR[k] = grp_tile(sb)
-                gw = words_of(GR[k])
-                xt = bank("s")
-                xv = xt[:].rearrange("p (i u n) -> p i u n", i=2, u=2)
-                for i in range(2):
-                    rbw = RB[(k, 2 * half + i)][:].rearrange("n u p e -> n (u p e)").bitcast(F32)
-                    for e in range(2):
-                        nc.tensor.transpose(xv[:, i, e, :], rbw[:, 128 * e : 128 * e + 128], ident[:])
-                nc.scalar.copy(out=gw[:, 2 * half : 2 * half + 2], in_=xv.rearrange("p i u n -> p i n u"))
-
-            def planes_store(k):
-                g, n0, wd, route = PLAN[k]
-                cw = sb.tile([128, 512], U32, name="cw", tag="cw", bufs=2, align_bytes=64)
-                cs = sb.tile([128, 512], U8, name="cs", tag="cs", bufs=2, align_bytes=64)
-                quantize(cw[:, :wd], cs[:, :wd], GR[k][:, :wd, :])
-                nc.sync.dma_start(out=out_words[g].rearrange("p m t -> p (m t)").bitcast(I32)[:, n0 : n0 + wd], in_=cw[:, :wd].bitcast(I32))
-                for q in range(4):
-                    nc.sync.dma_start(
-                        out=out_scales[g, 4 * q : 4 * q + 4, :].bitcast(I32)[:, n0 // 4 : n0 // 4 + wd // 4],
-                        in_=cs[32 * q : 32 * q + 4, :wd].bitcast(I32),
-                    )
-
-            prep_u(0, "vs")
-            prep_w(0, "v")
-            prep_w(1, "v")
+            front_u(0, "vs")
+            front_w(0, "v")
+            front_w(1, "v")
             for t in range(4):
-                open_y(0, t)
+                open_cell(0, t)
             for p in range(NP):
-                prep_q(p, 0, "ssss")
-                prep_v(p, 0, "ss")
-                if p + 2 < NP:
-                    prep_w(p + 2, "v")
+                front_q(p, 0)
                 if p > 0:
-                    for t in range(4):
+                    flush()
+                    for t in range(2):
                         argument(0, t, p - 1)
-
-            prep_u(1, "ss")
+                flush()
+                front_v(p, 0)
+                if p > 0:
+                    for t in range(2, 4):
+                        argument(0, t, p - 1)
+                if p < 2:
+                    front_w(p + 2, "gg"[p])
+            flush()
             for t in range(4):
                 argument(0, t, 3)
+                silu(0, t)
+            front_u(1, "vv")
+            shift_phase(
+                0,
+                [
+                    [lambda: front_q(0, 1)],
+                    [lambda: front_q(1, 1), flush],
+                    [lambda: front_q(2, 1), flush],
+                    [lambda: front_q(3, 1), flush, flush],
+                ],
+            )
+            weigh_phase(0)
+            shift_phase(1, [[], [], [lambda: front_v(0, 1), lambda: front_v(1, 1)], [lambda: front_v(2, 1), lambda: front_v(3, 1)]])
+            flush(4)
 
-            for t in range(4):
-                for p in range(NP):
-                    silu(0, t, p)
-                prep_q(t, 1, "ssss")
-            for t in range(4):
-                prep_v(t, 1, "ss")
-        pool_of["late"] = ctx.enter_context(tc.tile_pool(name="late", bufs=1))
-
-        def logs(k):
-            for j in range(PLAN[k][2] // 128):
-                recip_a(k, j)
-            for j in range(PLAN[k][2] // 128):
-                recip_b(k, j)
-
-        cells = [(k, i) for k in range(len(PLAN)) for i in range(ncells(k))]
-        fills = []
-
-        def fill(n):
-            for _ in range(n):
-                if fills:
-                    fills.pop(0)()
-
-        def queue_mixes(k):
-            nj = PLAN[k][2] // 128
-            for j in range(nj):
-                fills.append(lambda j=j: mix(k, j))
-                if j == nj - 1 or j % 2 == 1:
-                    fills.append(lambda j=j: planes_turn(k, j // 2))
-            fills.append(lambda: planes_store(k))
-
-        def queue_weigh(k):
-            for t in range(4):
-                for p in range(NP):
-                    fills.append(lambda t=t, p=p: weigh(k, t, p))
-
-        LATE = [9, 4, 4, 4]
-        FL = [(0, 0), (4, 2), (4, 2), (4, 2)]
-
-        early = set()
-
-        def args(k, i, n):
-            open_y(k, i)
-            early.add((k, i))
-            for p in range(NP):
-                argument(k, i, p)
-                if p >= NP - n:
-                    fill(1)
-
-        def head(k, i, n):
-            if (k, i) not in early:
-                args(k, i, n)
-            else:
-                fill(n)
-            for p in range(NP):
-                silu(k, i, p)
-
-        def rest(k, i, n):
-            max_a(k, i)
-            fill(1 if n > 0 else 0)
-            max_b(k, i)
-            fill(1 if n > 1 else 0)
-            if PLAN[k][3] == "d":
-                for p in range(NP):
-                    shift(k, i, p)
-
-        for s, (k, i) in enumerate(cells):
-            f = FL[i * 4 // ncells(k)] if k > 0 else (0, 0)
-            nxt = cells[s + 1] if s + 1 < len(cells) else None
-            lastc = i == ncells(k) - 1
-            if lastc and k > 0 and LATE[k] == 4:
-                fill(99)
-                logs(k - 1)
-                queue_mixes(k - 1)
-            if nxt and nxt[0] > 0 and not lastc:
-                head(nxt[0], nxt[1], f[0])
-            rest(k, i, f[1])
-            if k > 0 and i == LATE[k]:
-                logs(k - 1)
-            if lastc:
-                if k > 0 and LATE[k] != 4:
-                    fill(99)
-                    queue_mixes(k - 1)
-                for c in cells[s + 1 : s + 1 + (1 if PLAN[k][3] == "d" else 2)]:
-                    if c[0] == k + 1:
-                        args(c[0], c[1], 0)
-                if PLAN[k][3] == "d":
-                    for t in range(4):
-                        expo(k, t)
-                if nxt:
-                    head(nxt[0], nxt[1], 0)
-
-                queue_weigh(k)
-        fill(99)
-        logs(len(PLAN) - 1)
-        queue_mixes(len(PLAN) - 1)
-        fill(99)
+        late.append(ctx.enter_context(tc.tile_pool(name="late", bufs=1)))
+        weigh_phase(1)
+        for k in range(2, len(BATCHES)):
+            shift_phase(k, [[], [], [], []])
+            weigh_phase(k)
+        for j in range(4):
+            mix(last, j)
+            if j % 2 == 1:
+                planes_turn(last, j // 2)
+        planes_store(last)

@@ -17,269 +17,331 @@ N = 1024
 M = 1024
 D = 512
 K = 512
-C_MIN = 1e-20
 FLOPS = 2 * NP * N * D * K + 2 * NP * N * M * K
 
-BATCHES = ((0, 0), (0, 512), (1, 512), (1, 0))
+P = 128
+HALF = 512
+C_MIN = 1e-20
+
+BATCHES = ((0, 0), (0, HALF), (1, HALF), (1, 0))
+LAST = len(BATCHES) - 1
+
+LOGIT_BANKS = 4
+OTHER_BANKS = 4
+
+
+def copy_on_vector(nc, dst, src):
+    nc.vector.tensor_copy(out=dst, in_=src)
+
+
+def copy_on_scalar(nc, dst, src):
+    nc.scalar.copy(out=dst, in_=src)
+
+
+def copy_on_gpsimd(nc, dst, src):
+    nc.gpsimd.tensor_scalar(out=dst, in0=src, scalar1=1.0, scalar2=0.0, op0=ALU.mult, op1=ALU.add)
+
+
+def as_words(grouped):
+    return grouped[:].rearrange("p x f -> p (x f)").bitcast(F32).rearrange("p (i n e) -> p i n e", n=P, e=2)
+
+
+def quantize(nc, codes, scales, grouped):
+    nc.vector.quantize_mx(out=codes.bitcast(FP8X4), scales=scales, in_=grouped[:].rearrange("p x f -> p (x f)"))
 
 
 def tile_mixtureoflogitsretrievalscore_x1_kernel(tc, u, w, v, a, b, c, out, out_words, out_scales):
     nc = tc.nc
     with ExitStack() as ctx:
         keep = ctx.enter_context(tc.tile_pool(name="keep", bufs=1))
-        sb = ctx.enter_context(tc.tile_pool(name="sb", bufs=2))
-        ps = ctx.enter_context(tc.psum_pool(name="ps", bufs=5))
+        work = ctx.enter_context(tc.tile_pool(name="work", bufs=2))
+        psum = ctx.enter_context(tc.psum_pool(name="psum", bufs=OTHER_BANKS))
         ctx.enter_context(tc.manual_schedule())
 
         def logit_bank():
-            acc = ps.tile([128, 512], F32, name="logit", tag="logit", bufs=5)
-            return acc
+            bank = psum.tile([P, HALF], F32, name="logit", tag="logit", bufs=LOGIT_BANKS)
+            return bank
 
         def other_bank():
-            acc = ps.tile([128, 512], F32, name="other", tag="other", bufs=3)
-            return acc
+            bank = psum.tile([P, HALF], F32, name="other", tag="other", bufs=OTHER_BANKS)
+            return bank
 
-        ident = keep.tile([128, 128], F32)
+        ident = keep.tile([P, P], F32)
         make_identity(nc, ident[:])
 
-        c_b = keep.tile([128, NP], BF16)
-        nc.scalar.dma_start(out=c_b[:], in_=c.partition_broadcast(128))
-        b_b = keep.tile([128, 2, 4 * NP], BF16)
-        nc.scalar.dma_start(out=b_b[:], in_=b.rearrange("(g p t) c -> p g (t c)", p=128, t=4))
-        a_all = keep.tile([128, N, NP], BF16)
+        a_all = keep.tile([P, N, NP], BF16)
+        c_raw = keep.tile([P, NP], BF16)
+        nc.scalar.dma_start(out=c_raw[:], in_=c.partition_broadcast(P))
+        b_raw = keep.tile([P, 2, 4 * NP], BF16)
+        nc.scalar.dma_start(out=b_raw[:], in_=b.rearrange("(g p t) c -> p g (t c)", p=P, t=4))
 
-        q_q = keep.tile([128, NP, N], U32, align_bytes=64)
-        q_s = keep.tile([128, NP, N], U8, align_bytes=64)
-        v_q = keep.tile([128, NP, M], U32, align_bytes=64)
-        v_s = keep.tile([128, NP, M], U8, align_bytes=64)
+        q_codes = keep.tile([P, NP, N], U32, align_bytes=64)
+        q_scales = keep.tile([P, NP, N], U8, align_bytes=64)
+        v_codes = keep.tile([P, NP, M], U32, align_bytes=64)
+        v_scales = keep.tile([P, NP, M], U8, align_bytes=64)
 
-        def load_a():
-            nc.sync.dma_start(out=a_all[:].rearrange("q n c -> q (n c)"), in_=a.rearrange("n c -> (n c)").partition_broadcast(128))
-
-        c_f = keep.tile([128, NP], F32)
-        nc.vector.tensor_copy(out=c_f[:], in_=c_b[:])
-        b_f = keep.tile([128, 8, NP], F32)
-        nc.vector.tensor_copy(out=b_f[:].rearrange("p x c -> p (x c)"), in_=b_b[:].rearrange("p g x -> p (g x)"))
-        c_abs = keep.tile([128, NP], F32)
-        nc.vector.scalar_tensor_tensor(out=c_abs[:], in0=c_f[:], scalar=-1.0, in1=c_f[:], op0=ALU.mult, op1=ALU.max)
-        c_fill = keep.tile([128, NP], F32)
+        c_safe = keep.tile([P, NP], F32)
+        nc.vector.tensor_copy(out=c_safe[:], in_=c_raw[:])
+        b_f32 = keep.tile([P, 8, NP], F32)
+        nc.vector.tensor_copy(out=b_f32[:].rearrange("p x c -> p (x c)"), in_=b_raw[:].rearrange("p g x -> p (g x)"))
+        c_abs = keep.tile([P, NP], F32)
+        nc.vector.scalar_tensor_tensor(out=c_abs[:], in0=c_safe[:], scalar=-1.0, in1=c_safe[:], op0=ALU.mult, op1=ALU.max)
+        c_fill = keep.tile([P, NP], F32)
         nc.vector.tensor_scalar(out=c_fill[:], in0=c_abs[:], scalar1=C_MIN, scalar2=C_MIN, op0=ALU.is_lt, op1=ALU.mult)
-        c_big = keep.tile([128, NP], F32)
+        c_big = keep.tile([P, NP], F32)
         nc.vector.tensor_scalar(out=c_big[:], in0=c_abs[:], scalar1=C_MIN, scalar2=None, op0=ALU.is_ge)
-        nc.vector.tensor_tensor(out=c_f[:], in0=c_f[:], in1=c_big[:], op=ALU.mult)
-        nc.vector.tensor_tensor(out=c_f[:], in0=c_f[:], in1=c_fill[:], op=ALU.add)
-        c_inv = keep.tile([128, NP], F32)
-        nc.vector.reciprocal(out=c_inv[:], in_=c_f[:])
-        b_over_c = keep.tile([128, 8, NP], F32)
-        nc.vector.tensor_tensor(out=b_over_c[:], in0=b_f[:], in1=c_inv[:].unsqueeze(1).to_broadcast([128, 8, NP]), op=ALU.mult)
+        nc.vector.tensor_tensor(out=c_safe[:], in0=c_safe[:], in1=c_big[:], op=ALU.mult)
+        nc.vector.tensor_tensor(out=c_safe[:], in0=c_safe[:], in1=c_fill[:], op=ALU.add)
+        c_inv = keep.tile([P, NP], F32)
+        nc.vector.reciprocal(out=c_inv[:], in_=c_safe[:])
+        b_over_c = keep.tile([P, 8, NP], F32)
+        nc.vector.tensor_tensor(out=b_over_c[:], in0=b_f32[:], in1=c_inv[:].unsqueeze(1).to_broadcast([P, 8, NP]), op=ALU.mult)
 
-        def quantize(codes, scales, grouped):
-            nc.vector.quantize_mx(out=codes.bitcast(FP8X4), scales=scales, in_=grouped[:].rearrange("p n f -> p (n f)"))
+        cell = {}
+        pair_max, maximum = {}, {}
+        weighed = {}
+        e_pair = {}
+        e_sum, el_sum = {}, {}
+        inverse = {}
+        rounded = {}
+        planes = {}
+        pools = {}
 
-        def as_words(grouped):
-            return grouped[:].rearrange("p n f -> p (n f)").bitcast(F32).rearrange("p (i n e) -> p i n e", n=128, e=2)
-
-        def copy(engine, dst, src):
-            if engine == "v":
-                nc.vector.tensor_copy(out=dst, in_=src)
-            elif engine == "s":
-                nc.scalar.copy(out=dst, in_=src)
-            else:
-                nc.gpsimd.tensor_scalar(out=dst, in0=src, scalar1=1.0, scalar2=0.0, op0=ALU.mult, op1=ALU.add)
-
-        Y, E, EL, SH, ZS, RZ, RB, GR = {}, {}, {}, {}, {}, {}, {}, {}
-        late = []
-
-        def mx_logits(k, t, p):
+        def logits(k, t, p):
             g, n0 = BATCHES[k]
-            m0 = 512 * g + 128 * t
-            acc = logit_bank()
+            m0 = HALF * g + P * t
+            bank = logit_bank()
             nc.tensor.matmul_mx(
-                out=acc[:],
-                lhsT=v_q[:, p, m0 : m0 + 128].bitcast(FP8X4),
-                lhsT_scale=v_s[:, p, m0 : m0 + 128],
-                rhs=q_q[:, p, n0 : n0 + 512].bitcast(FP8X4),
-                rhs_scale=q_s[:, p, n0 : n0 + 512],
+                out=bank[:],
+                lhsT=v_codes[:, p, m0 : m0 + P].bitcast(FP8X4),
+                lhsT_scale=v_scales[:, p, m0 : m0 + P],
+                rhs=q_codes[:, p, n0 : n0 + HALF].bitcast(FP8X4),
+                rhs_scale=q_scales[:, p, n0 : n0 + HALF],
                 start=True,
                 stop=True,
             )
-            return acc
+            return bank
 
         def open_cell(k, t):
             if k == 2:
-                y = late[0].tile([128, NP, 512], F32, name="y2", tag="y2", bufs=4)
+                tile = pools["late"].tile([P, NP, HALF], F32, name="cell2", tag="cell2", bufs=4)
             else:
-                y = sb.tile([128, NP, 512], F32, name="y", tag="y%d" % (k % 3), bufs=4)
-            Y[k, t] = y
+                tile = work.tile([P, NP, HALF], F32, name="cell", tag="cell%d" % (k % 3), bufs=4)
+            cell[k, t] = tile
 
         def argument(k, t, p):
             g, n0 = BATCHES[k]
-            acc = mx_logits(k, t, p)
+            bank = logits(k, t, p)
             nc.vector.scalar_tensor_tensor(
-                out=Y[k, t][:, p, :], in0=a_all[:, n0 : n0 + 512, p], scalar=b_over_c[:, 4 * g + t, p : p + 1], in1=acc[:], op0=ALU.mult, op1=ALU.add
+                out=cell[k, t][:, p, :],
+                in0=a_all[:, n0 : n0 + HALF, p],
+                scalar=b_over_c[:, 4 * g + t, p : p + 1],
+                in1=bank[:],
+                op0=ALU.mult,
+                op1=ALU.add,
             )
 
         def silu(k, t):
             for p in range(NP):
-                y = Y[k, t][:, p, :]
-                nc.scalar.activation(out=y, in_=y, func=ACT.Silu, scale=c_f[:, p : p + 1])
+                x = cell[k, t][:, p, :]
+                nc.scalar.activation(out=x, in_=x, func=ACT.Silu, scale=c_safe[:, p : p + 1])
 
-        def max_pairs(k, t):
-            y = Y[k, t]
-            m2 = sb.tile([128, 2, 512], F32, name="m2", tag="m2", bufs=1)
-            nc.vector.tensor_tensor(out=m2[:], in0=y[:, 0:2, :], in1=y[:, 2:4, :], op=ALU.max)
-            SH[k, t] = m2
+        def max_of_pairs(k, t):
+            x = cell[k, t]
+            tile = work.tile([P, 2, HALF], F32, name="pair_max", tag="pair_max", bufs=1)
+            nc.vector.tensor_tensor(out=tile[:], in0=x[:, 0:2, :], in1=x[:, 2:4, :], op=ALU.max)
+            pair_max[k, t] = tile
 
-        def max_all(k, t):
-            m2 = SH[k, t]
-            s = sb.tile([128, 512], F32, name="s", tag="s", bufs=3)
-            nc.vector.tensor_tensor(out=s[:], in0=m2[:, 0, :], in1=m2[:, 1, :], op=ALU.max)
-            SH[k, t] = s
+        def max_of_all(k, t):
+            m2 = pair_max[k, t]
+            tile = work.tile([P, HALF], F32, name="maximum", tag="maximum", bufs=3)
+            nc.vector.tensor_tensor(out=tile[:], in0=m2[:, 0, :], in1=m2[:, 1, :], op=ALU.max)
+            maximum[k, t] = tile
 
-        def shift(k, t):
-            for p in range(NP):
-                engine = nc.gpsimd if t in (3,) else nc.vector
-                y = Y[k, t][:, p, :]
-                engine.tensor_tensor(out=y, in0=y, in1=SH[k, t][:], op=ALU.subtract)
+        def shifted_on_gpsimd(k, t):
+            return t == 3 and k < LAST
 
-        def expo(k, t):
-            nc.scalar.activation(out=Y[k, t][:], in_=Y[k, t][:], func=ACT.Exp)
+        def subtract_maximum(k, t, components):
+            engine = nc.gpsimd if shifted_on_gpsimd(k, t) else nc.vector
+            for p in components:
+                x = cell[k, t][:, p, :]
+                engine.tensor_tensor(out=x, in0=x, in1=maximum[k, t][:], op=ALU.subtract)
+
+        def exponential(k, t):
+            nc.scalar.activation(out=cell[k, t][:], in_=cell[k, t][:], func=ACT.Exp)
 
         def weigh(k, t):
-            el = sb.tile([128, NP, 512], F32, name="el", tag="el", bufs=4)
-            EL[k, t] = el
+            tile = work.tile([P, NP, HALF], F32, name="weighed", tag="weighed", bufs=4)
+            weighed[k, t] = tile
             for p in range(NP):
-                acc = mx_logits(k, t, p)
-                nc.vector.tensor_tensor(out=el[:, p, :], in0=acc[:], in1=Y[k, t][:, p, :], op=ALU.mult)
+                bank = logits(k, t, p)
+                nc.vector.tensor_tensor(out=tile[:, p, :], in0=bank[:], in1=cell[k, t][:, p, :], op=ALU.mult)
 
-        def sum_components(cells, k, j):
-            acc = other_bank()
+        def add_up(bank, parts, j, t):
+            count = parts.shape[1]
+            for i in range(count):
+                nc.tensor.matmul(
+                    out=bank[:, P * t : P * t + P],
+                    lhsT=parts[:, i, P * j : P * j + P],
+                    rhs=ident[:],
+                    is_transpose=True,
+                    start=(i == 0),
+                    stop=(i == count - 1),
+                )
+
+        def sum_e(k, j):
+            bank = other_bank()
+            e_sum[k, j] = bank
             for t in range(4):
-                for p in range(NP):
-                    nc.tensor.matmul(
-                        out=acc[:, 128 * t : 128 * t + 128],
-                        lhsT=cells[k, t][:, p, 128 * j : 128 * j + 128],
-                        rhs=ident[:],
-                        is_transpose=True,
-                        start=(p == 0),
-                        stop=(p == NP - 1),
-                    )
-            return acc
+                add_up(bank, cell[k, t], j, t)
 
-        def z_sum(k, j):
-            ZS[k, j] = sum_components(Y, k, j)
+        def sum_weighed(k, j):
+            bank = other_bank()
+            el_sum[k, j] = bank
+            for t in range(4):
+                add_up(bank, weighed[k, t], j, t)
 
-        def reciprocals(k):
+        def invert_sums(k):
             for j in range(4):
-                if (k, j) not in ZS:
-                    z_sum(k, j)
-                rz = sb.tile([128, 512], F32, name="rz", tag="rz", bufs=4)
-                RZ[k, j] = rz
-                nc.scalar.activation(out=rz[:].rearrange("n (p t) -> n p t", t=4), in_=ZS[k, j][:].rearrange("n (t p) -> n p t", t=4), func=ACT.Ln)
+                tile = work.tile([P, HALF], F32, name="inverse", tag="inverse", bufs=4)
+                inverse[k, j] = tile
+                nc.scalar.activation(
+                    out=tile[:].rearrange("n (p t) -> n p t", t=4), in_=e_sum[k, j][:].rearrange("n (t p) -> n p t", t=4), func=ACT.Ln
+                )
             for j in range(4):
-                nc.scalar.activation(out=RZ[k, j][:], in_=RZ[k, j][:], func=ACT.Exp, scale=-1.0)
+                nc.scalar.activation(out=inverse[k, j][:], in_=inverse[k, j][:], func=ACT.Exp, scale=-1.0)
 
         def mix(k, j):
             g, n0 = BATCHES[k]
-            num = sum_components(EL, k, j)
-            r = sb.tile([128, 512], F32, name="r", tag="r", bufs=2)
+            tile = work.tile([P, HALF], F32, name="result", tag="result", bufs=2)
             nc.vector.tensor_tensor(
-                out=r[:].rearrange("n (p t) -> n p t", t=4),
-                in0=num[:].rearrange("n (t p) -> n p t", t=4),
-                in1=RZ[k, j][:].rearrange("n (p t) -> n p t", t=4),
+                out=tile[:].rearrange("n (p t) -> n p t", t=4),
+                in0=el_sum[k, j][:].rearrange("n (t p) -> n p t", t=4),
+                in1=inverse[k, j][:].rearrange("n (p t) -> n p t", t=4),
                 op=ALU.mult,
             )
-            n1 = n0 + 128 * j
-            nc.sync.dma_start(out=out[n1 : n1 + 128, 512 * g : 512 * g + 512], in_=r[:])
-            rb = sb.tile([128, 2, 128, 2], BF16, name="rb", tag="rb", bufs=4)
-            RB[k, j] = rb
-            copy("g", rb[:], r[:].rearrange("n (p e f) -> n e p f", e=2, f=2))
+            n1 = n0 + P * j
+            nc.sync.dma_start(out=out[n1 : n1 + P, HALF * g : HALF * g + HALF], in_=tile[:])
+            half = work.tile([P, 2, P, 2], BF16, name="rounded", tag="rounded", bufs=4)
+            rounded[k, j] = half
+            copy_on_gpsimd(nc, half[:], tile[:].rearrange("n (p e f) -> n e p f", e=2, f=2))
 
-        def planes_turn(k, half):
-            if half == 0:
-                grouped = sb.tile([128, 512, 4], BF16, name="planes", tag="planes", bufs=2, align_bytes=64)
-                GR[k] = grouped
-            bank = other_bank()
-            view = bank[:].rearrange("p (i e n) -> p i e n", i=2, e=2)
-            for i in range(2):
-                words = RB[k, 2 * half + i][:].rearrange("n e p f -> n (e p f)").bitcast(F32)
-                for e in range(2):
-                    nc.tensor.transpose(view[:, i, e, :], words[:, 128 * e : 128 * e + 128], ident[:])
-            nc.scalar.copy(out=as_words(GR[k])[:, 2 * half : 2 * half + 2], in_=view.rearrange("p i e n -> p i n e"))
+        def turn_planes(k):
+            grouped = work.tile([P, HALF, 4], BF16, name="planes", tag="planes", bufs=2, align_bytes=64)
+            planes[k] = grouped
+            for pair in range(2):
+                bank = other_bank()
+                view = bank[:].rearrange("p (i e n) -> p i e n", i=2, e=2)
+                for i in range(2):
+                    words = rounded[k, 2 * pair + i][:].rearrange("n e p f -> n (e p f)").bitcast(F32)
+                    for e in range(2):
+                        nc.tensor.transpose(view[:, i, e, :], words[:, P * e : P * e + P], ident[:])
+                nc.scalar.copy(out=as_words(grouped)[:, 2 * pair : 2 * pair + 2], in_=view.rearrange("p i e n -> p i n e"))
 
-        def planes_store(k):
+        def store_planes(k):
             g, n0 = BATCHES[k]
-            codes = sb.tile([128, 512], U32, name="codes", tag="codes", bufs=2, align_bytes=64)
-            scales = sb.tile([128, 512], U8, name="scales", tag="scales", bufs=2, align_bytes=64)
-            quantize(codes[:], scales[:], GR[k])
-            nc.sync.dma_start(out=out_words[g].rearrange("p m t -> p (m t)").bitcast(I32)[:, n0 : n0 + 512], in_=codes[:].bitcast(I32))
+            codes = work.tile([P, HALF], U32, name="codes", tag="codes", bufs=2, align_bytes=64)
+            scales = work.tile([P, HALF], U8, name="scales", tag="scales", bufs=2, align_bytes=64)
+            quantize(nc, codes[:], scales[:], planes[k])
+            nc.sync.dma_start(out=out_words[g].rearrange("p m t -> p (m t)").bitcast(I32)[:, n0 : n0 + HALF], in_=codes[:].bitcast(I32))
             for q in range(4):
                 nc.sync.dma_start(
-                    out=out_scales[g, 4 * q : 4 * q + 4, :].bitcast(I32)[:, n0 // 4 : n0 // 4 + 128],
+                    out=out_scales[g, 4 * q : 4 * q + 4, :].bitcast(I32)[:, n0 // 4 : (n0 + HALF) // 4],
                     in_=scales[32 * q : 32 * q + 4, :].bitcast(I32),
                 )
 
-        last = len(BATCHES) - 1
+        def shift_phase(k, after_cell):
+            for t in range(5):
+                late_cell = t > 0 and not shifted_on_gpsimd(k, t - 1)
+                mixing = k > 0 and t in (2, 3)
+                if t < 4:
+                    max_of_pairs(k, t)
+                if late_cell:
+                    subtract_maximum(k, t - 1, (0, 1))
+                if mixing:
+                    sum_weighed(k - 1, 2 * (t - 2))
+                    mix(k - 1, 2 * (t - 2))
+                if t < 4:
+                    max_of_all(k, t)
+                    if shifted_on_gpsimd(k, t):
+                        subtract_maximum(k, t, range(NP))
+                if late_cell:
+                    subtract_maximum(k, t - 1, (2, 3))
+                if mixing:
+                    sum_weighed(k - 1, 2 * (t - 2) + 1)
+                    mix(k - 1, 2 * (t - 2) + 1)
+                if t > 0:
+                    after_cell(t - 1)
 
-        def shift_phase(k, front):
-            todo = []
-            for t in range(4):
-                if k > 0 and t == 2:
-                    todo = [0, 1, 2, 3]
-                max_pairs(k, t)
-                if todo:
-                    mix(k - 1, todo.pop(0))
-                max_all(k, t)
-                if todo:
-                    mix(k - 1, todo.pop(0))
-                shift(k, t)
-                for f in front[t]:
-                    f()
-            for j in todo:
-                mix(k - 1, j)
+        def nothing(t):
+            return None
 
         def weigh_phase(k):
             for t in range(4):
-                expo(k, t)
+                exponential(k, t)
             for t in range(4):
-                if k < last:
-                    open_cell(k + 1, t)
-                    for p in range(NP):
-                        argument(k + 1, t, p)
+                open_cell(k + 1, t)
+                for p in range(NP):
+                    argument(k + 1, t, p)
                 if k > 0 and t == 1:
-                    planes_turn(k - 1, 0)
-                    planes_turn(k - 1, 1)
-                if k > 0 and t == 3:
-                    planes_store(k - 1)
+                    turn_planes(k - 1)
                 if t == 3:
-                    if k == last:
-                        reciprocals(k)
-                    else:
-                        z_sum(k, 0)
+                    if k > 0:
+                        store_planes(k - 1)
+                    sum_e(k, 0)
                 weigh(k, t)
-            if k < last:
-                for j in (1, 2):
-                    z_sum(k, j)
-                for t in range(4):
-                    silu(k + 1, t)
-                reciprocals(k)
+            for j in range(1, 4):
+                sum_e(k, j)
+            for t in range(4):
+                silu(k + 1, t)
+            invert_sums(k)
 
-        with tc.tile_pool(name="front", bufs=1) as fr:
-            raws = {}
+        def last_phase(k):
+            for t in range(4):
+                exponential(k, t)
+                tile = pools["late"].tile([P, 2, HALF], F32, name="e_pair", tag="e_pair", bufs=4)
+                e_pair[k, t] = tile
+                nc.gpsimd.tensor_tensor(out=tile[:], in0=cell[k, t][:, 0:2, :], in1=cell[k, t][:, 2:4, :], op=ALU.add)
+                if t == 0:
+                    turn_planes(k - 1)
+            for j in range(4):
+                e_sum[k, j] = other_bank()
+            for t in range(5):
+                if t < 4:
+                    weigh(k, t)
+                if t == 1:
+                    store_planes(k - 1)
+                if t > 0:
+                    for j in range(4):
+                        add_up(e_sum[k, j], e_pair[k, t - 1], j, t - 1)
+                    for j in range(2):
+                        if t == 1:
+                            el_sum[k, j] = logit_bank()
+                        add_up(el_sum[k, j], weighed[k, t - 1], j, t - 1)
+            invert_sums(k)
+            for j in range(2, 4):
+                sum_weighed(k, j)
+            for j in range(4):
+                mix(k, j)
+            turn_planes(k)
+            store_planes(k)
 
-            def load(key, src):
-                raw = fr.tile([128, 4, 512], BF16, name="raw", tag="raw", bufs=5)
-                nc.sync.dma_start(out=raw[:], in_=src)
-                raws[key] = raw
+        with tc.tile_pool(name="front", bufs=1) as front:
+            raw = {}
+
+            def load(name, src):
+                tile = front.tile([P, 4, HALF], BF16, name="raw", tag="raw", bufs=5)
+                nc.sync.dma_start(out=tile[:], in_=src)
+                raw[name] = tile
 
             def load_u(h):
-                load(("u", h), u[512 * h : 512 * h + 512, :].rearrange("(i p) d -> p i d", p=128))
+                load(("u", h), u[HALF * h : HALF * h + HALF, :].rearrange("(i p) d -> p i d", p=P))
 
             def load_w(p):
                 load(("w", p), w[p].rearrange("(p j) c -> p j c", j=4))
 
             def load_v(p, g):
-                load(("v", p, g), v[p, 512 * g : 512 * g + 512, :].rearrange("(p t) k -> p t k", t=4))
+                load(("v", p, g), v[p, HALF * g : HALF * g + HALF, :].rearrange("(p t) k -> p t k", t=4))
 
             load_u(0)
             load_w(0)
@@ -287,7 +349,7 @@ def tile_mixtureoflogitsretrievalscore_x1_kernel(tc, u, w, v, a, b, c, out, out_
             load_w(1)
             load_v(1, 0)
             load_w(2)
-            load_a()
+            nc.sync.dma_start(out=a_all[:].rearrange("q n c -> q (n c)"), in_=a.rearrange("n c -> (n c)").partition_broadcast(P))
             load_v(2, 0)
             load_w(3)
             load_v(3, 0)
@@ -295,110 +357,110 @@ def tile_mixtureoflogitsretrievalscore_x1_kernel(tc, u, w, v, a, b, c, out, out_
             for p in range(NP):
                 load_v(p, 1)
 
-            u_q = fr.tile([128, N], U32, align_bytes=64)
-            u_s = fr.tile([128, N], U8, align_bytes=64)
-            w_q = fr.tile([128, NP, K], U32, align_bytes=64)
-            w_s = fr.tile([128, NP, K], U8, align_bytes=64)
+            u_codes = front.tile([P, N], U32, align_bytes=64)
+            u_scales = front.tile([P, N], U8, align_bytes=64)
+            w_codes = front.tile([P, NP, K], U32, align_bytes=64)
+            w_scales = front.tile([P, NP, K], U8, align_bytes=64)
+            to_quantize = []
 
-            def front_group():
-                grouped = fr.tile([128, 512, 4], BF16, name="grouped", tag="grouped", bufs=4, align_bytes=64)
-                return grouped
+            def quantize_next():
+                codes, scales, grouped = to_quantize.pop(0)
+                quantize(nc, codes, scales, grouped)
 
-            def turn(raw, engine):
-                grouped = front_group()
-                words = raw[:].rearrange("p i k -> p (i k)").bitcast(F32)
-                for half in range(2):
+            def grouped_tile():
+                tile = front.tile([P, HALF, 4], BF16, name="grouped", tag="grouped", bufs=4, align_bytes=64)
+                return tile
+
+            def turn(tile, copies):
+                grouped = grouped_tile()
+                words = tile[:].rearrange("p i k -> p (i k)").bitcast(F32)
+                for pair in range(2):
                     bank = other_bank()
                     view = bank[:].rearrange("p (i e n) -> p i e n", i=2, e=2)
                     for i in range(2):
                         for e in range(2):
-                            base = 256 * (2 * half + i)
-                            nc.tensor.transpose(view[:, i, e, :], words[:, base + e : base + 256 : 2], ident[:])
-                    copy(engine[half], as_words(grouped)[:, 2 * half : 2 * half + 2], view.rearrange("p i e n -> p i n e"))
+                            first = 256 * (2 * pair + i)
+                            nc.tensor.transpose(view[:, i, e, :], words[:, first + e : first + 256 : 2], ident[:])
+                    copies[pair](nc, as_words(grouped)[:, 2 * pair : 2 * pair + 2], view.rearrange("p i e n -> p i n e"))
                 return grouped
 
-            def front_u(h, engine):
-                grouped = turn(raws["u", h], engine)
-                quantize(u_q[:, 512 * h : 512 * h + 512], u_s[:, 512 * h : 512 * h + 512], grouped)
+            def turn_u(h, copies):
+                grouped = turn(raw["u", h], copies)
+                quantize(nc, u_codes[:, HALF * h : HALF * h + HALF], u_scales[:, HALF * h : HALF * h + HALF], grouped)
 
-            def front_w(p, engine):
-                grouped = front_group()
-                dst = grouped[:].rearrange("p x f -> p (x f)").rearrange("p (t m j) -> p t m j", t=4, j=4)
-                copy(engine, dst, raws["w", p][:].rearrange("p j (m t) -> p t m j", t=4))
-                quantize(w_q[:, p, :], w_s[:, p, :], grouped)
+            def turn_v(p, g):
+                grouped = turn(raw["v", p, g], (copy_on_scalar, copy_on_scalar))
+                cols = slice(HALF * g, HALF * g + HALF)
+                to_quantize.append((v_codes[:, p, cols], v_scales[:, p, cols], grouped))
 
-            pending = []
+            def group_w(p, copy):
+                grouped = grouped_tile()
+                dst = grouped[:].rearrange("p x f -> p (x f)").rearrange("p (t x j) -> p t x j", t=4, j=4)
+                copy(nc, dst, raw["w", p][:].rearrange("p j (x t) -> p t x j", t=4))
+                quantize(nc, w_codes[:, p, :], w_scales[:, p, :], grouped)
 
-            def front_q(p, h, engine="ssss"):
-                grouped = front_group()
+            def project(p, h):
+                grouped = grouped_tile()
                 for i in range(4):
                     bank = other_bank()
                     view = bank[:].rearrange("p (t n) -> p t n", t=4)
-                    n0 = 512 * h + 128 * i
+                    n0 = HALF * h + P * i
                     for t in range(4):
                         nc.tensor.matmul_mx(
                             out=view[:, t, :],
-                            lhsT=w_q[:, p, 128 * t : 128 * t + 128].bitcast(FP8X4),
-                            lhsT_scale=w_s[:, p, 128 * t : 128 * t + 128],
-                            rhs=u_q[:, n0 : n0 + 128].bitcast(FP8X4),
-                            rhs_scale=u_s[:, n0 : n0 + 128],
+                            lhsT=w_codes[:, p, P * t : P * t + P].bitcast(FP8X4),
+                            lhsT_scale=w_scales[:, p, P * t : P * t + P],
+                            rhs=u_codes[:, n0 : n0 + P].bitcast(FP8X4),
+                            rhs_scale=u_scales[:, n0 : n0 + P],
                             start=True,
                             stop=True,
                         )
-                    copy(engine[i], grouped[:, 128 * i : 128 * i + 128, :], view.rearrange("p t n -> p n t"))
-                pending.append((q_q[:, p, 512 * h : 512 * h + 512], q_s[:, p, 512 * h : 512 * h + 512], grouped))
+                    copy_on_scalar(nc, grouped[:, P * i : P * i + P, :], view.rearrange("p t n -> p n t"))
+                cols = slice(HALF * h, HALF * h + HALF)
+                to_quantize.append((q_codes[:, p, cols], q_scales[:, p, cols], grouped))
 
-            def front_v(p, g, engine="ss"):
-                grouped = turn(raws["v", p, g], engine)
-                pending.append((v_q[:, p, 512 * g : 512 * g + 512], v_s[:, p, 512 * g : 512 * g + 512], grouped))
-
-            def flush(n=1):
-                for _ in range(n):
-                    quantize(*pending.pop(0))
-
-            front_u(0, "vs")
-            front_w(0, "v")
-            front_w(1, "v")
+            turn_u(0, (copy_on_vector, copy_on_scalar))
+            for p in range(2):
+                group_w(p, copy_on_vector)
             for t in range(4):
                 open_cell(0, t)
             for p in range(NP):
-                front_q(p, 0)
+                project(p, 0)
                 if p > 0:
-                    flush()
-                    for t in range(2):
+                    quantize_next()
+                    for t in range(4):
                         argument(0, t, p - 1)
-                flush()
-                front_v(p, 0)
-                if p > 0:
-                    for t in range(2, 4):
-                        argument(0, t, p - 1)
-                if p < 2:
-                    front_w(p + 2, "gg"[p])
-            flush()
+                quantize_next()
+                turn_v(p, 0)
+                if p + 2 < NP:
+                    group_w(p + 2, copy_on_gpsimd)
+            quantize_next()
             for t in range(4):
                 argument(0, t, 3)
                 silu(0, t)
-            front_u(1, "vv")
-            shift_phase(
-                0,
-                [
-                    [lambda: front_q(0, 1)],
-                    [lambda: front_q(1, 1), flush],
-                    [lambda: front_q(2, 1), flush],
-                    [lambda: front_q(3, 1), flush, flush],
-                ],
-            )
-            weigh_phase(0)
-            shift_phase(1, [[], [], [lambda: front_v(0, 1), lambda: front_v(1, 1)], [lambda: front_v(2, 1), lambda: front_v(3, 1)]])
-            flush(4)
+            turn_u(1, (copy_on_vector, copy_on_vector))
 
-        late.append(ctx.enter_context(tc.tile_pool(name="late", bufs=1)))
+            def project_other_queries(t):
+                project(t, 1)
+                if t > 0:
+                    quantize_next()
+                if t == 3:
+                    quantize_next()
+
+            def turn_other_items(t):
+                if t >= 2:
+                    turn_v(2 * (t - 2), 1)
+                    turn_v(2 * (t - 2) + 1, 1)
+
+            shift_phase(0, project_other_queries)
+            weigh_phase(0)
+            shift_phase(1, turn_other_items)
+            for p in range(NP):
+                quantize_next()
+
+        pools["late"] = ctx.enter_context(tc.tile_pool(name="late", bufs=1))
         weigh_phase(1)
-        for k in range(2, len(BATCHES)):
-            shift_phase(k, [[], [], [], []])
-            weigh_phase(k)
-        for j in range(4):
-            mix(last, j)
-            if j % 2 == 1:
-                planes_turn(last, j // 2)
-        planes_store(last)
+        shift_phase(2, nothing)
+        weigh_phase(2)
+        shift_phase(3, nothing)
+        last_phase(3)

from contextlib import ExitStack

import concourse.mybir as mybir
from concourse.masks import make_identity

F32 = mybir.dt.float32
BF16 = mybir.dt.bfloat16
U32 = mybir.dt.uint32
I32 = mybir.dt.int32
U8 = mybir.dt.uint8
FP8X4 = mybir.dt.float8_e4m3fn_x4
ALU = mybir.AluOpType
ACT = mybir.ActivationFunctionType

NP = 4
N = 1024
M = 1024
D = 512
K = 512
FLOPS = 2 * NP * N * D * K + 2 * NP * N * M * K

P = 128
HALF = 512
C_MIN = 1e-20

BATCHES = ((0, 0), (0, HALF), (1, HALF), (1, 0))
LAST = len(BATCHES) - 1

LOGIT_BANKS = 4
OTHER_BANKS = 4


def copy_on_vector(nc, dst, src):
    nc.vector.tensor_copy(out=dst, in_=src)


def copy_on_scalar(nc, dst, src):
    nc.scalar.copy(out=dst, in_=src)


def copy_on_gpsimd(nc, dst, src):
    nc.gpsimd.tensor_scalar(out=dst, in0=src, scalar1=1.0, scalar2=0.0, op0=ALU.mult, op1=ALU.add)


def as_words(grouped):
    return grouped[:].rearrange("p x f -> p (x f)").bitcast(F32).rearrange("p (i n e) -> p i n e", n=P, e=2)


def quantize(nc, codes, scales, grouped):
    nc.vector.quantize_mx(out=codes.bitcast(FP8X4), scales=scales, in_=grouped[:].rearrange("p x f -> p (x f)"))


def tile_mixtureoflogitsretrievalscore_x1_kernel(tc, u, w, v, a, b, c, out, out_words, out_scales):
    nc = tc.nc
    with ExitStack() as ctx:
        keep = ctx.enter_context(tc.tile_pool(name="keep", bufs=1))
        work = ctx.enter_context(tc.tile_pool(name="work", bufs=2))
        psum = ctx.enter_context(tc.psum_pool(name="psum", bufs=OTHER_BANKS))
        ctx.enter_context(tc.manual_schedule())

        def logit_bank():
            bank = psum.tile([P, HALF], F32, name="logit", tag="logit", bufs=LOGIT_BANKS)
            return bank

        def other_bank():
            bank = psum.tile([P, HALF], F32, name="other", tag="other", bufs=OTHER_BANKS)
            return bank

        ident = keep.tile([P, P], F32)
        make_identity(nc, ident[:])

        a_all = keep.tile([P, N, NP], BF16)
        c_raw = keep.tile([P, NP], BF16)
        nc.scalar.dma_start(out=c_raw[:], in_=c.partition_broadcast(P))
        b_raw = keep.tile([P, 2, 4 * NP], BF16)
        nc.scalar.dma_start(out=b_raw[:], in_=b.rearrange("(g p t) c -> p g (t c)", p=P, t=4))

        q_codes = keep.tile([P, NP, N], U32, align_bytes=64)
        q_scales = keep.tile([P, NP, N], U8, align_bytes=64)
        v_codes = keep.tile([P, NP, M], U32, align_bytes=64)
        v_scales = keep.tile([P, NP, M], U8, align_bytes=64)

        c_safe = keep.tile([P, NP], F32)
        nc.vector.tensor_copy(out=c_safe[:], in_=c_raw[:])
        b_f32 = keep.tile([P, 8, NP], F32)
        nc.vector.tensor_copy(out=b_f32[:].rearrange("p x c -> p (x c)"), in_=b_raw[:].rearrange("p g x -> p (g x)"))
        c_abs = keep.tile([P, NP], F32)
        nc.vector.scalar_tensor_tensor(out=c_abs[:], in0=c_safe[:], scalar=-1.0, in1=c_safe[:], op0=ALU.mult, op1=ALU.max)
        c_fill = keep.tile([P, NP], F32)
        nc.vector.tensor_scalar(out=c_fill[:], in0=c_abs[:], scalar1=C_MIN, scalar2=C_MIN, op0=ALU.is_lt, op1=ALU.mult)
        c_big = keep.tile([P, NP], F32)
        nc.vector.tensor_scalar(out=c_big[:], in0=c_abs[:], scalar1=C_MIN, scalar2=None, op0=ALU.is_ge)
        nc.vector.tensor_tensor(out=c_safe[:], in0=c_safe[:], in1=c_big[:], op=ALU.mult)
        nc.vector.tensor_tensor(out=c_safe[:], in0=c_safe[:], in1=c_fill[:], op=ALU.add)
        c_inv = keep.tile([P, NP], F32)
        nc.vector.reciprocal(out=c_inv[:], in_=c_safe[:])
        b_over_c = keep.tile([P, 8, NP], F32)
        nc.vector.tensor_tensor(out=b_over_c[:], in0=b_f32[:], in1=c_inv[:].unsqueeze(1).to_broadcast([P, 8, NP]), op=ALU.mult)

        cell = {}
        pair_max, maximum = {}, {}
        weighed = {}
        e_pair = {}
        e_sum, el_sum = {}, {}
        inverse = {}
        rounded = {}
        planes = {}
        pools = {}

        def logits(k, t, p):
            g, n0 = BATCHES[k]
            m0 = HALF * g + P * t
            bank = logit_bank()
            nc.tensor.matmul_mx(
                out=bank[:],
                lhsT=v_codes[:, p, m0 : m0 + P].bitcast(FP8X4),
                lhsT_scale=v_scales[:, p, m0 : m0 + P],
                rhs=q_codes[:, p, n0 : n0 + HALF].bitcast(FP8X4),
                rhs_scale=q_scales[:, p, n0 : n0 + HALF],
                start=True,
                stop=True,
            )
            return bank

        def open_cell(k, t):
            if k == 2:
                tile = pools["late"].tile([P, NP, HALF], F32, name="cell2", tag="cell2", bufs=4)
            else:
                tile = work.tile([P, NP, HALF], F32, name="cell", tag="cell%d" % (k % 3), bufs=4)
            cell[k, t] = tile

        def argument(k, t, p):
            g, n0 = BATCHES[k]
            bank = logits(k, t, p)
            nc.vector.scalar_tensor_tensor(
                out=cell[k, t][:, p, :],
                in0=a_all[:, n0 : n0 + HALF, p],
                scalar=b_over_c[:, 4 * g + t, p : p + 1],
                in1=bank[:],
                op0=ALU.mult,
                op1=ALU.add,
            )

        def silu(k, t):
            for p in range(NP):
                x = cell[k, t][:, p, :]
                nc.scalar.activation(out=x, in_=x, func=ACT.Silu, scale=c_safe[:, p : p + 1])

        def max_of_pairs(k, t):
            x = cell[k, t]
            tile = work.tile([P, 2, HALF], F32, name="pair_max", tag="pair_max", bufs=1)
            nc.vector.tensor_tensor(out=tile[:], in0=x[:, 0:2, :], in1=x[:, 2:4, :], op=ALU.max)
            pair_max[k, t] = tile

        def max_of_all(k, t):
            m2 = pair_max[k, t]
            tile = work.tile([P, HALF], F32, name="maximum", tag="maximum", bufs=3)
            nc.vector.tensor_tensor(out=tile[:], in0=m2[:, 0, :], in1=m2[:, 1, :], op=ALU.max)
            maximum[k, t] = tile

        def shifted_on_gpsimd(k, t):
            return t == 3 and k < LAST

        def subtract_maximum(k, t, components):
            engine = nc.gpsimd if shifted_on_gpsimd(k, t) else nc.vector
            for p in components:
                x = cell[k, t][:, p, :]
                engine.tensor_tensor(out=x, in0=x, in1=maximum[k, t][:], op=ALU.subtract)

        def exponential(k, t):
            nc.scalar.activation(out=cell[k, t][:], in_=cell[k, t][:], func=ACT.Exp)

        def weigh(k, t):
            tile = work.tile([P, NP, HALF], F32, name="weighed", tag="weighed", bufs=4)
            weighed[k, t] = tile
            for p in range(NP):
                bank = logits(k, t, p)
                nc.vector.tensor_tensor(out=tile[:, p, :], in0=bank[:], in1=cell[k, t][:, p, :], op=ALU.mult)

        def add_up(bank, parts, j, t):
            count = parts.shape[1]
            for i in range(count):
                nc.tensor.matmul(
                    out=bank[:, P * t : P * t + P],
                    lhsT=parts[:, i, P * j : P * j + P],
                    rhs=ident[:],
                    is_transpose=True,
                    start=(i == 0),
                    stop=(i == count - 1),
                )

        def sum_e(k, j):
            bank = other_bank()
            e_sum[k, j] = bank
            for t in range(4):
                add_up(bank, cell[k, t], j, t)

        def sum_weighed(k, j):
            bank = other_bank()
            el_sum[k, j] = bank
            for t in range(4):
                add_up(bank, weighed[k, t], j, t)

        def invert_sums(k):
            for j in range(4):
                tile = work.tile([P, HALF], F32, name="inverse", tag="inverse", bufs=4)
                inverse[k, j] = tile
                nc.scalar.activation(
                    out=tile[:].rearrange("n (p t) -> n p t", t=4), in_=e_sum[k, j][:].rearrange("n (t p) -> n p t", t=4), func=ACT.Ln
                )
            for j in range(4):
                nc.scalar.activation(out=inverse[k, j][:], in_=inverse[k, j][:], func=ACT.Exp, scale=-1.0)

        def mix(k, j):
            g, n0 = BATCHES[k]
            tile = work.tile([P, HALF], F32, name="result", tag="result", bufs=2)
            nc.vector.tensor_tensor(
                out=tile[:].rearrange("n (p t) -> n p t", t=4),
                in0=el_sum[k, j][:].rearrange("n (t p) -> n p t", t=4),
                in1=inverse[k, j][:].rearrange("n (p t) -> n p t", t=4),
                op=ALU.mult,
            )
            n1 = n0 + P * j
            nc.sync.dma_start(out=out[n1 : n1 + P, HALF * g : HALF * g + HALF], in_=tile[:])
            half = work.tile([P, 2, P, 2], BF16, name="rounded", tag="rounded", bufs=4)
            rounded[k, j] = half
            copy_on_gpsimd(nc, half[:], tile[:].rearrange("n (p e f) -> n e p f", e=2, f=2))

        def turn_planes(k):
            grouped = work.tile([P, HALF, 4], BF16, name="planes", tag="planes", bufs=2, align_bytes=64)
            planes[k] = grouped
            for pair in range(2):
                bank = other_bank()
                view = bank[:].rearrange("p (i e n) -> p i e n", i=2, e=2)
                for i in range(2):
                    words = rounded[k, 2 * pair + i][:].rearrange("n e p f -> n (e p f)").bitcast(F32)
                    for e in range(2):
                        nc.tensor.transpose(view[:, i, e, :], words[:, P * e : P * e + P], ident[:])
                nc.scalar.copy(out=as_words(grouped)[:, 2 * pair : 2 * pair + 2], in_=view.rearrange("p i e n -> p i n e"))

        def store_planes(k):
            g, n0 = BATCHES[k]
            codes = work.tile([P, HALF], U32, name="codes", tag="codes", bufs=2, align_bytes=64)
            scales = work.tile([P, HALF], U8, name="scales", tag="scales", bufs=2, align_bytes=64)
            quantize(nc, codes[:], scales[:], planes[k])
            nc.sync.dma_start(out=out_words[g].rearrange("p m t -> p (m t)").bitcast(I32)[:, n0 : n0 + HALF], in_=codes[:].bitcast(I32))
            for q in range(4):
                nc.sync.dma_start(
                    out=out_scales[g, 4 * q : 4 * q + 4, :].bitcast(I32)[:, n0 // 4 : (n0 + HALF) // 4],
                    in_=scales[32 * q : 32 * q + 4, :].bitcast(I32),
                )

        def shift_phase(k, after_cell):
            for t in range(5):
                late_cell = t > 0 and not shifted_on_gpsimd(k, t - 1)
                mixing = k > 0 and t in (2, 3)
                if t < 4:
                    max_of_pairs(k, t)
                if late_cell:
                    subtract_maximum(k, t - 1, (0, 1))
                if mixing:
                    sum_weighed(k - 1, 2 * (t - 2))
                    mix(k - 1, 2 * (t - 2))
                if t < 4:
                    max_of_all(k, t)
                    if shifted_on_gpsimd(k, t):
                        subtract_maximum(k, t, range(NP))
                if late_cell:
                    subtract_maximum(k, t - 1, (2, 3))
                if mixing:
                    sum_weighed(k - 1, 2 * (t - 2) + 1)
                    mix(k - 1, 2 * (t - 2) + 1)
                if t > 0:
                    after_cell(t - 1)

        def nothing(t):
            return None

        def weigh_phase(k):
            for t in range(4):
                exponential(k, t)
            for t in range(4):
                open_cell(k + 1, t)
                for p in range(NP):
                    argument(k + 1, t, p)
                if k > 0 and t == 1:
                    turn_planes(k - 1)
                if t == 3:
                    if k > 0:
                        store_planes(k - 1)
                    sum_e(k, 0)
                weigh(k, t)
            for j in range(1, 4):
                sum_e(k, j)
            for t in range(4):
                silu(k + 1, t)
            invert_sums(k)

        def last_phase(k):
            for t in range(4):
                exponential(k, t)
                tile = pools["late"].tile([P, 2, HALF], F32, name="e_pair", tag="e_pair", bufs=4)
                e_pair[k, t] = tile
                nc.gpsimd.tensor_tensor(out=tile[:], in0=cell[k, t][:, 0:2, :], in1=cell[k, t][:, 2:4, :], op=ALU.add)
                if t == 0:
                    turn_planes(k - 1)
            for j in range(4):
                e_sum[k, j] = other_bank()
            for t in range(5):
                if t < 4:
                    weigh(k, t)
                if t == 1:
                    store_planes(k - 1)
                if t > 0:
                    for j in range(4):
                        add_up(e_sum[k, j], e_pair[k, t - 1], j, t - 1)
                    for j in range(2):
                        if t == 1:
                            el_sum[k, j] = logit_bank()
                        add_up(el_sum[k, j], weighed[k, t - 1], j, t - 1)
            invert_sums(k)
            for j in range(2, 4):
                sum_weighed(k, j)
            for j in range(4):
                mix(k, j)
            turn_planes(k)
            store_planes(k)

        with tc.tile_pool(name="front", bufs=1) as front:
            raw = {}

            def load(name, src):
                tile = front.tile([P, 4, HALF], BF16, name="raw", tag="raw", bufs=5)
                nc.sync.dma_start(out=tile[:], in_=src)
                raw[name] = tile

            def load_u(h):
                load(("u", h), u[HALF * h : HALF * h + HALF, :].rearrange("(i p) d -> p i d", p=P))

            def load_w(p):
                load(("w", p), w[p].rearrange("(p j) c -> p j c", j=4))

            def load_v(p, g):
                load(("v", p, g), v[p, HALF * g : HALF * g + HALF, :].rearrange("(p t) k -> p t k", t=4))

            load_u(0)
            load_w(0)
            load_v(0, 0)
            load_w(1)
            load_v(1, 0)
            load_w(2)
            nc.sync.dma_start(out=a_all[:].rearrange("q n c -> q (n c)"), in_=a.rearrange("n c -> (n c)").partition_broadcast(P))
            load_v(2, 0)
            load_w(3)
            load_v(3, 0)
            load_u(1)
            for p in range(NP):
                load_v(p, 1)

            u_codes = front.tile([P, N], U32, align_bytes=64)
            u_scales = front.tile([P, N], U8, align_bytes=64)
            w_codes = front.tile([P, NP, K], U32, align_bytes=64)
            w_scales = front.tile([P, NP, K], U8, align_bytes=64)
            to_quantize = []

            def quantize_next():
                codes, scales, grouped = to_quantize.pop(0)
                quantize(nc, codes, scales, grouped)

            def grouped_tile():
                tile = front.tile([P, HALF, 4], BF16, name="grouped", tag="grouped", bufs=4, align_bytes=64)
                return tile

            def turn(tile, copies):
                grouped = grouped_tile()
                words = tile[:].rearrange("p i k -> p (i k)").bitcast(F32)
                for pair in range(2):
                    bank = other_bank()
                    view = bank[:].rearrange("p (i e n) -> p i e n", i=2, e=2)
                    for i in range(2):
                        for e in range(2):
                            first = 256 * (2 * pair + i)
                            nc.tensor.transpose(view[:, i, e, :], words[:, first + e : first + 256 : 2], ident[:])
                    copies[pair](nc, as_words(grouped)[:, 2 * pair : 2 * pair + 2], view.rearrange("p i e n -> p i n e"))
                return grouped

            def turn_u(h, copies):
                grouped = turn(raw["u", h], copies)
                quantize(nc, u_codes[:, HALF * h : HALF * h + HALF], u_scales[:, HALF * h : HALF * h + HALF], grouped)

            def turn_v(p, g):
                grouped = turn(raw["v", p, g], (copy_on_scalar, copy_on_scalar))
                cols = slice(HALF * g, HALF * g + HALF)
                to_quantize.append((v_codes[:, p, cols], v_scales[:, p, cols], grouped))

            def group_w(p, copy):
                grouped = grouped_tile()
                dst = grouped[:].rearrange("p x f -> p (x f)").rearrange("p (t x j) -> p t x j", t=4, j=4)
                copy(nc, dst, raw["w", p][:].rearrange("p j (x t) -> p t x j", t=4))
                quantize(nc, w_codes[:, p, :], w_scales[:, p, :], grouped)

            def project(p, h):
                grouped = grouped_tile()
                for i in range(4):
                    bank = other_bank()
                    view = bank[:].rearrange("p (t n) -> p t n", t=4)
                    n0 = HALF * h + P * i
                    for t in range(4):
                        nc.tensor.matmul_mx(
                            out=view[:, t, :],
                            lhsT=w_codes[:, p, P * t : P * t + P].bitcast(FP8X4),
                            lhsT_scale=w_scales[:, p, P * t : P * t + P],
                            rhs=u_codes[:, n0 : n0 + P].bitcast(FP8X4),
                            rhs_scale=u_scales[:, n0 : n0 + P],
                            start=True,
                            stop=True,
                        )
                    copy_on_scalar(nc, grouped[:, P * i : P * i + P, :], view.rearrange("p t n -> p n t"))
                cols = slice(HALF * h, HALF * h + HALF)
                to_quantize.append((q_codes[:, p, cols], q_scales[:, p, cols], grouped))

            turn_u(0, (copy_on_vector, copy_on_scalar))
            for p in range(2):
                group_w(p, copy_on_vector)
            for t in range(4):
                open_cell(0, t)
            for p in range(NP):
                project(p, 0)
                if p > 0:
                    quantize_next()
                    for t in range(4):
                        argument(0, t, p - 1)
                quantize_next()
                turn_v(p, 0)
                if p + 2 < NP:
                    group_w(p + 2, copy_on_gpsimd)
            quantize_next()
            for t in range(4):
                argument(0, t, 3)
                silu(0, t)
            turn_u(1, (copy_on_vector, copy_on_vector))

            def project_other_queries(t):
                project(t, 1)
                if t > 0:
                    quantize_next()
                if t == 3:
                    quantize_next()

            def turn_other_items(t):
                if t >= 2:
                    turn_v(2 * (t - 2), 1)
                    turn_v(2 * (t - 2) + 1, 1)

            shift_phase(0, project_other_queries)
            weigh_phase(0)
            shift_phase(1, turn_other_items)
            for p in range(NP):
                quantize_next()

        pools["late"] = ctx.enter_context(tc.tile_pool(name="late", bufs=1))
        weigh_phase(1)
        shift_phase(2, nothing)
        weigh_phase(2)
        shift_phase(3, nothing)
        last_phase(3)
